import numpy as np
import ml_dtypes


def mxq(x, axis, fmt="e4m3"):
    dtype, down = {"e4m3": (ml_dtypes.float8_e4m3fn, 7), "e5m2": (ml_dtypes.float8_e5m2, 14)}[fmt]
    v = np.moveaxis(np.asarray(x, np.float32).astype(ml_dtypes.bfloat16).astype(np.float64), axis, -1)
    blocks = v.reshape(v.shape[:-1] + (-1, 32))
    amax = np.abs(blocks).max(-1, keepdims=True)
    byte = np.maximum(np.where(amax > 0, np.frexp(amax)[1] - 1 + 127, 0) - down, 1)
    scale = np.exp2(byte - 127.0)
    codes = (blocks / scale).astype(np.float32).astype(dtype).astype(np.float64)
    return np.moveaxis((codes * scale).reshape(v.shape), -1, axis)


WIDE = False


def mx_kscale(k):
    if not WIDE:
        return np.ones(k)
    levels = np.array([10, -10, 5, -5, 0])
    if k % 512:
        return np.exp2(np.random.permutation(np.resize(levels, k // 32))).repeat(32)
    a = np.empty((k // 512, 16))
    for p in range(k // 512):
        a[p, :8] = np.random.permutation(np.resize(levels, 8))
        for g in range(8):
            far = levels[np.abs(levels - a[p, g]) >= 10]
            a[p, g + 8] = far[np.random.randint(len(far))]
    return np.exp2(a.ravel()).repeat(32)


def f64(x):
    return np.asarray(x).astype(np.float64)


def striped(idx):
    return np.tile(idx.reshape(-1, 16).T, (8, 1)).astype(np.uint16)


def unstriped(offs):
    return offs[:16].T.reshape(-1).astype(np.int64)


def pack_weight(w):
    k, n = w.shape
    w = f64(np.asarray(w, np.float32).astype(ml_dtypes.bfloat16)).reshape(k // 32, 32, n)
    amax = np.abs(w).max(1)
    byte = np.clip(np.where(amax > 0, np.frexp(amax)[1] - 1 + 127 - 7, 1), 1, 254)
    scaled = (w * np.exp2(127.0 - byte)[:, None, :]).reshape(k, n).astype(np.float32)
    words = np.ascontiguousarray(scaled.reshape(k // 512, 128, 4, n).transpose(0, 1, 3, 2)).astype(ml_dtypes.float8_e4m3fn).view(np.uint8)
    return words, np.ascontiguousarray(byte.astype(np.uint8).reshape(k // 512, 16, n))


def unpack_weight(words, scales):
    g, p, n, _ = words.shape
    vals = np.ascontiguousarray(words).view(ml_dtypes.float8_e4m3fn).astype(np.float64) * np.repeat(np.exp2(scales.astype(np.float64) - 127.0), 8, axis=1)[..., None]
    return vals.transpose(0, 1, 3, 2).reshape(g * 512, n)


def planes(y):
    n, m = y.shape
    v = y.astype(np.float32).astype(ml_dtypes.bfloat16).astype(np.float64).reshape(n // 32, 32, m)
    top = np.abs(v).max(1)
    byte = np.clip(np.where(top > 0, np.frexp(top)[1] - 1 + 127 - 7, 1), 1, 254)
    codes = (v * np.exp2(127.0 - byte)[:, None, :]).reshape(n, m).astype(np.float32).astype(ml_dtypes.float8_e4m3fn).view(np.uint8)
    words = codes.reshape(n // 512, 128, 4, m).transpose(0, 1, 3, 2)
    return np.ascontiguousarray(words), np.ascontiguousarray(byte.astype(np.uint8).reshape(n // 512, 16, m))


def sigmoid(v):
    return 1.0 / (1.0 + np.exp(-np.maximum(v, -700.0)))


K, T, S, H = 1024, 2048, 1024, 512


def setup_inputs():
    n = np.random.standard_normal
    s = mx_kscale(K)[:, None]
    u = mx_kscale(H)
    packed_xT = pack_weight(n((K, T)) * s)
    return {
        "x_words": packed_xT[0],
        "x_scales": packed_xT[1],
        "w1": (n((K, H)) / np.sqrt(K) / s * u).astype(np.float32),
        "w2": (n((H, H)) / np.sqrt(H) / u[:, None]).astype(np.float32),
        "offs": striped(np.random.permutation(T)[:S]),
    }


def reference(x_words, x_scales, w1, w2, offs):
    xq = unpack_weight(x_words, x_scales)[:, unstriped(offs)]
    h = mxq(f64(w1), 0, "e4m3").T @ xq
    g = sigmoid(mxq(f64(w2), 0, "e4m3").T @ mxq(h, 0, "e4m3"))
    out_0 = h * g
    return (out_0,) + planes(out_0)

@@ -1,0 +1,202 @@
+from contextlib import ExitStack
+
+import concourse.mybir as mybir
+
+K, T, S, H = 1024, 2048, 1024, 512
+FLOPS = 2 * K * H * S + 2 * H * H * S
+
+F32 = mybir.dt.float32
+BF16 = mybir.dt.bfloat16
+I32 = mybir.dt.int32
+U32 = mybir.dt.uint32
+U16 = mybir.dt.uint16
+U8 = mybir.dt.uint8
+FP8X4 = mybir.dt.float8_e4m3fn_x4
+SIGMOID = mybir.ActivationFunctionType.Sigmoid
+MULT = mybir.AluOpType.mult
+
+P = 128
+PACK = 4
+K_PASS = P * PACK
+CHUNK = 128
+CHUNKS = S // CHUNK
+PIECE = 256
+W2_PARTS = ((0, 48), (48, 128))
+FIRST_SCALAR = 4
+SCALAR_CASTS = (5, 6)
+
+
+def tile_picked_zgrn_lin_po_kernel(tc, x_words, x_scales, w1, w2, offs, out_0, out_1, out_2):
+    nc = tc.nc
+    with ExitStack() as ctx:
+        keep = ctx.enter_context(tc.tile_pool(name="keep", bufs=1))
+        ring = ctx.enter_context(tc.tile_pool(name="ring", bufs=8))
+        psum_h = ctx.enter_context(tc.psum_pool(name="psum_h", bufs=5))
+        psum_z = ctx.enter_context(tc.psum_pool(name="psum_z", bufs=3))
+
+        offsets = keep.tile([P, S // 16], U16, name="offsets")
+        x_table = [keep.tile([P, T], U32, name="x_table%d" % g, align_bytes=64) for g in range(2)]
+        s_table = keep.tile([P, T], U8, name="s_table", align_bytes=64)
+        w_raw = [keep.tile([P, PACK, H], F32, name="w_raw%d" % g, tag="stage%d" % g, align_bytes=64) for g in range(2)]
+        w2_raw = [
+            keep.tile([P, PACK, PACK * (m1 - m0)], F32, name="w2_raw%d" % i, tag="w2_stage%d" % i, align_bytes=64)
+            for i, (m0, m1) in enumerate(W2_PARTS)
+        ]
+        w_bf = [keep.tile([P, PACK * H], BF16, name="w_bf%d" % g, align_bytes=64) for g in range(3)]
+        w_codes = [keep.tile([P, H], U32, name="w_codes%d" % g, align_bytes=64) for g in range(3)]
+        w_scales = [keep.tile([P, H], U8, name="w_scales%d" % g, align_bytes=64) for g in range(3)]
+        x_codes = [keep.tile([P, S], U32, name="x_codes%d" % g, align_bytes=64) for g in range(2)]
+        x_planes = keep.tile([P, S], U8, name="x_planes", align_bytes=64)
+        y_codes = keep.tile([P, S], U32, name="y_codes", align_bytes=64)
+        y_scales = keep.tile([P, S], U8, name="y_scales", align_bytes=64)
+
+        def load_x(g):
+            nc.sync.dma_start(out=x_table[g][:].bitcast(I32), in_=x_words[g].rearrange("p n t -> p (n t)").bitcast(I32))
+
+        def load_w(g, rows):
+            nc.sync.dma_start(out=w_raw[g][:], in_=rows.rearrange("(p j) c -> p j c", j=PACK))
+
+        nc.vector.memset(s_table[:].bitcast(I32), 0)
+        for half in range(2):
+            cols = slice(half * T // 2, (half + 1) * T // 2)
+            nc.sync.dma_start(out=x_table[0][:, cols].bitcast(I32), in_=x_words[0].rearrange("p n t -> p (n t)").bitcast(I32)[:, cols])
+        nc.sync.dma_start(offsets[:], offs)
+        for q in range(4):
+            nc.sync.dma_start(out=s_table[32 * q : 32 * q + 8, :].bitcast(I32), in_=x_scales[:, 4 * q : 4 * q + 4, :].bitcast(I32))
+        load_w(0, w1[0:K_PASS, :])
+        load_w(1, w1[K_PASS:K, :])
+        load_x(1)
+        for i, (m0, m1) in enumerate(W2_PARTS):
+            nc.sync.dma_start(out=w2_raw[i][:], in_=w2.rearrange("(p j) c -> p j c", j=PACK)[:, :, PACK * m0 : PACK * m1])
+
+        def deal(copy, g, m0, m1):
+            dst = w_bf[g][:].rearrange("p (t m j) -> p m j t", t=PACK, j=PACK)
+            src = w_raw[g][:].rearrange("p j (m t) -> p m j t", t=PACK)
+            copy(out=dst[:, m0:m1], in_=src[:, m0:m1])
+
+        def deal_w2(copy, i):
+            m0, m1 = W2_PARTS[i]
+            dst = w_bf[2][:].rearrange("p (t m j) -> p m j t", t=PACK, j=PACK)
+            copy(out=dst[:, m0:m1], in_=w2_raw[i][:].rearrange("p j (m t) -> p m j t", t=PACK))
+
+        def quantize_w(g):
+            nc.vector.quantize_mx(out=w_codes[g][:].bitcast(FP8X4), scales=w_scales[g][:], in_=w_bf[g][:])
+
+        nc.vector.tensor_copy(out=x_codes[0][:], in_=x_table[0][:].indirect(offsets[:]))
+        deal(nc.scalar.copy, 0, 0, 128)
+        nc.vector.tensor_copy(out=x_planes[:], in_=s_table[:].indirect(offsets[:]))
+        quantize_w(0)
+        deal(nc.scalar.copy, 1, 0, 80)
+        deal(nc.vector.tensor_copy, 1, 80, 128)
+        quantize_w(1)
+        for i in range(S // PIECE):
+            nc.vector.tensor_copy(
+                out=x_codes[1][:, i * PIECE : (i + 1) * PIECE],
+                in_=x_table[1][:].indirect(offsets[:, i * PIECE // 16 : (i + 1) * PIECE // 16]),
+            )
+
+        h_ps, h_q, gate = {}, {}, {}
+        y_rows = out_0.rearrange("(p t) n -> p t n", t=PACK)
+        y_words = out_1[0].rearrange("p n t -> p (n t)").bitcast(I32)
+
+        def first_product(c):
+            cols = slice(c * CHUNK, (c + 1) * CHUNK)
+            h_ps[c] = psum_h.tile([P, PACK, CHUNK], F32, name="h")
+            for t in range(PACK):
+                for g in range(2):
+                    nc.tensor.matmul_mx(
+                        out=h_ps[c][:, t, :],
+                        lhsT=w_codes[g][:, t * P : (t + 1) * P].bitcast(FP8X4),
+                        lhsT_scale=w_scales[g][:, t * P : (t + 1) * P],
+                        rhs=x_codes[g][:, cols].bitcast(FP8X4),
+                        rhs_scale=x_planes[4 * g : P, cols],
+                        start=(g == 0),
+                        stop=(g == 1),
+                    )
+
+        y, y_bf = {}, {}
+
+        def round_h(c):
+            run = h_bf[:, c * CHUNK * PACK : (c + 1) * CHUNK * PACK]
+            nc.scalar.copy(out=run.rearrange("p (n t) -> p n t", t=PACK), in_=h_ps[c][:].rearrange("p t n -> p n t"))
+
+        def quantize_h(c):
+            cols = slice(c * CHUNK, (c + 1) * CHUNK)
+            nc.vector.quantize_mx(out=h_codes[:, cols].bitcast(FP8X4), scales=h_scales[:, cols], in_=h_bf[:, c * CHUNK * PACK : (c + 1) * CHUNK * PACK])
+
+        def second_product(c):
+            z = psum_z.tile([P, PACK, CHUNK], F32, name="z")
+            cols = slice(c * CHUNK, (c + 1) * CHUNK)
+            for t in range(PACK):
+                nc.tensor.matmul_mx(
+                    out=z[:, t, :],
+                    lhsT=w_codes[2][:, t * P : (t + 1) * P].bitcast(FP8X4),
+                    lhsT_scale=w_scales[2][:, t * P : (t + 1) * P],
+                    rhs=h_codes[:, cols].bitcast(FP8X4),
+                    rhs_scale=h_scales[:, cols],
+                    start=True,
+                    stop=True,
+                )
+            gate[c] = ring.tile([P, PACK, CHUNK], F32, name="gate", align_bytes=64)
+            nc.scalar.activation(out=gate[c][:], in_=z[:], func=SIGMOID)
+
+        def gate_h(c):
+            cols = slice(c * CHUNK, (c + 1) * CHUNK)
+            y[c] = ring.tile([P, PACK, CHUNK], F32, name="y", align_bytes=64)
+            nc.vector.tensor_tensor(out=y[c][:], in0=h_ps[c][:], in1=gate[c][:], op=MULT)
+            nc.sync.dma_start(out=y_rows[:, :, cols], in_=y[c][:])
+
+        def round_y(c):
+            y_bf[c] = ring.tile([P, CHUNK * PACK], BF16, name="y_bf", align_bytes=64)
+            dst = y_bf[c][:].rearrange("p (c i t) -> p c t i", i=4, t=PACK)
+            src = y[c][:].rearrange("p t (c i) -> p c t i", i=4)
+            if c == CHUNKS - 1:
+                nc.scalar.copy(out=dst[:, 0:12], in_=src[:, 0:12])
+                nc.vector.tensor_copy(out=dst[:, 12:32], in_=src[:, 12:32])
+            elif c >= FIRST_SCALAR:
+                nc.scalar.copy(out=dst, in_=src)
+            else:
+                nc.vector.tensor_copy(out=dst, in_=src)
+
+        def quantize_y(c):
+            cols = slice(c * CHUNK, (c + 1) * CHUNK)
+            nc.vector.quantize_mx(out=y_codes[:, cols].bitcast(FP8X4), scales=y_scales[:, cols], in_=y_bf[c][:])
+            if c % 2 == 1:
+                two = slice((c - 1) * CHUNK, (c + 1) * CHUNK)
+                nc.sync.dma_start(out=y_words[:, two], in_=y_codes[:, two].bitcast(I32))
+
+        deal_w2(nc.scalar.copy, 0)
+        h_bf = keep.tile([P, S * PACK], BF16, name="h_bf", tag="w2_stage0", align_bytes=64)
+        AHEAD = 5
+        for c in range(AHEAD):
+            first_product(c)
+            round_h(c)
+        deal_w2(nc.vector.tensor_copy, 1)
+        h_codes = keep.tile([P, S], U32, name="h_codes", tag="w2_stage1", align_bytes=64)
+        h_scales = keep.tile([P, S], U8, name="h_scales", align_bytes=64)
+        quantize_h(0)
+        quantize_w(2)
+        quantize_h(1)
+        for c in range(CHUNKS):
+            second_product(c)
+            if c + 2 < CHUNKS:
+                quantize_h(c + 2)
+            if c == CHUNKS - 1:
+                round_y(FIRST_SCALAR)
+                quantize_y(FIRST_SCALAR)
+            gate_h(c)
+            if c + AHEAD < CHUNKS:
+                first_product(c + AHEAD)
+                round_h(c + AHEAD)
+            if 0 <= c - 2 < FIRST_SCALAR:
+                quantize_y(c - 2)
+            if 0 <= c - 1 < FIRST_SCALAR:
+                round_y(c - 1)
+        for c in range(FIRST_SCALAR + 1, CHUNKS):
+            round_y(c)
+            if c > FIRST_SCALAR + 1:
+                quantize_y(c - 1)
+        quantize_y(CHUNKS - 1)
+        for q in range(4):
+            queue = nc.sync if q % 2 == 0 else nc.scalar
+            queue.dma_start(out=out_2[0, 4 * q : 4 * q + 4, :].bitcast(I32), in_=y_scales[32 * q : 32 * q + 4, :].bitcast(I32))

@@ -68,6 +68,9 @@ def tile_picked_zgrn_lin_po_kernel(tc, x_words, x_scales, w1, w2, offs, out_0, o
         load_x(1)
         for i, (m0, m1) in enumerate(W2_PARTS):
             nc.sync.dma_start(out=w2_raw[i][:], in_=w2.rearrange("(p j) c -> p j c", j=PACK)[:, :, PACK * m0 : PACK * m1])
+        warm = keep.tile([P, 8], F32, name="warm")
+        nc.vector.memset(warm[:], 0.0)
+        nc.scalar.activation(out=warm[:], in_=warm[:], func=SIGMOID)
 
         def deal(copy, g, m0, m1):
             dst = w_bf[g][:].rearrange("p (t m j) -> p m j t", t=PACK, j=PACK)

@@ -18,125 +18,137 @@ MULT = mybir.AluOpType.mult
 P = 128
 PACK = 4
 K_PASS = P * PACK
+PASSES = K // K_PASS
+W2 = PASSES
+QUADRANTS = 4
+QUADRANT = P // QUADRANTS
+SCALE_ROWS = 4
+LIST_ROWS = 16
 CHUNK = 128
 CHUNKS = S // CHUNK
+LINE = 4
 PIECE = 256
-W2_PARTS = ((0, 48), (48, 128))
+
+H_BANKS = 5
+Z_BANKS = 3
+QUANTIZE_AHEAD = 2
+
+W1_SCALAR = (96, 64)
+W2_PARTS = ((0, 64), (64, P))
 FIRST_SCALAR = 4
-SCALAR_CASTS = (5, 6)
+LAST_SCALAR = 12
 
 
 def tile_picked_zgrn_lin_po_kernel(tc, x_words, x_scales, w1, w2, offs, out_0, out_1, out_2):
     nc = tc.nc
     with ExitStack() as ctx:
         keep = ctx.enter_context(tc.tile_pool(name="keep", bufs=1))
-        ring = ctx.enter_context(tc.tile_pool(name="ring", bufs=8))
-        psum_h = ctx.enter_context(tc.psum_pool(name="psum_h", bufs=5))
-        psum_z = ctx.enter_context(tc.psum_pool(name="psum_z", bufs=3))
+        ring = ctx.enter_context(tc.tile_pool(name="ring", bufs=CHUNKS))
+        psum_h = ctx.enter_context(tc.psum_pool(name="psum_h", bufs=H_BANKS))
+        psum_z = ctx.enter_context(tc.psum_pool(name="psum_z", bufs=Z_BANKS))
 
-        offsets = keep.tile([P, S // 16], U16, name="offsets")
-        x_table = [keep.tile([P, T], U32, name="x_table%d" % g, align_bytes=64) for g in range(2)]
+        offsets = keep.tile([P, S // LIST_ROWS], U16, name="offsets")
+        x_table = [keep.tile([P, T], U32, name="x_table%d" % g, align_bytes=64) for g in range(PASSES)]
         s_table = keep.tile([P, T], U8, name="s_table", align_bytes=64)
-        w_raw = [keep.tile([P, PACK, H], F32, name="w_raw%d" % g, tag="stage%d" % g, align_bytes=64) for g in range(2)]
+        w1_raw = [keep.tile([P, PACK, H], F32, name="w_raw%d" % g, tag="stage%d" % g, align_bytes=64) for g in range(PASSES)]
         w2_raw = [
             keep.tile([P, PACK, PACK * (m1 - m0)], F32, name="w2_raw%d" % i, tag="w2_stage%d" % i, align_bytes=64)
             for i, (m0, m1) in enumerate(W2_PARTS)
         ]
-        w_bf = [keep.tile([P, PACK * H], BF16, name="w_bf%d" % g, align_bytes=64) for g in range(3)]
-        w_codes = [keep.tile([P, H], U32, name="w_codes%d" % g, align_bytes=64) for g in range(3)]
-        w_scales = [keep.tile([P, H], U8, name="w_scales%d" % g, align_bytes=64) for g in range(3)]
-        x_codes = [keep.tile([P, S], U32, name="x_codes%d" % g, align_bytes=64) for g in range(2)]
+        w_bf = [keep.tile([P, PACK * H], BF16, name="w_bf%d" % g, align_bytes=64) for g in range(PASSES + 1)]
+        w_codes = [keep.tile([P, H], U32, name="w_codes%d" % g, align_bytes=64) for g in range(PASSES + 1)]
+        w_scales = [keep.tile([P, H], U8, name="w_scales%d" % g, align_bytes=64) for g in range(PASSES + 1)]
+        x_codes = [keep.tile([P, S], U32, name="x_codes%d" % g, align_bytes=64) for g in range(PASSES)]
         x_planes = keep.tile([P, S], U8, name="x_planes", align_bytes=64)
         y_codes = keep.tile([P, S], U32, name="y_codes", align_bytes=64)
         y_scales = keep.tile([P, S], U8, name="y_scales", align_bytes=64)
 
-        def load_x(g):
-            nc.sync.dma_start(out=x_table[g][:].bitcast(I32), in_=x_words[g].rearrange("p n t -> p (n t)").bitcast(I32))
-
-        def load_w(g, rows):
-            nc.sync.dma_start(out=w_raw[g][:], in_=rows.rearrange("(p j) c -> p j c", j=PACK))
-
+        x_rows = [x_words[g].rearrange("p n t -> p (n t)").bitcast(I32) for g in range(PASSES)]
         nc.vector.memset(s_table[:].bitcast(I32), 0)
         for half in range(2):
             cols = slice(half * T // 2, (half + 1) * T // 2)
-            nc.sync.dma_start(out=x_table[0][:, cols].bitcast(I32), in_=x_words[0].rearrange("p n t -> p (n t)").bitcast(I32)[:, cols])
+            nc.sync.dma_start(out=x_table[0][:, cols].bitcast(I32), in_=x_rows[0][:, cols])
         nc.sync.dma_start(offsets[:], offs)
-        for q in range(4):
-            nc.sync.dma_start(out=s_table[32 * q : 32 * q + 8, :].bitcast(I32), in_=x_scales[:, 4 * q : 4 * q + 4, :].bitcast(I32))
-        load_w(0, w1[0:K_PASS, :])
-        load_w(1, w1[K_PASS:K, :])
-        load_x(1)
+        for q in range(QUADRANTS):
+            nc.sync.dma_start(
+                out=s_table[QUADRANT * q : QUADRANT * q + PASSES * SCALE_ROWS, :].bitcast(I32),
+                in_=x_scales[:, SCALE_ROWS * q : SCALE_ROWS * (q + 1), :].bitcast(I32),
+            )
+        for g in range(PASSES):
+            nc.sync.dma_start(out=w1_raw[g][:], in_=w1[g * K_PASS : (g + 1) * K_PASS, :].rearrange("(p j) c -> p j c", j=PACK))
+        nc.sync.dma_start(out=x_table[1][:].bitcast(I32), in_=x_rows[1])
         for i, (m0, m1) in enumerate(W2_PARTS):
             nc.sync.dma_start(out=w2_raw[i][:], in_=w2.rearrange("(p j) c -> p j c", j=PACK)[:, :, PACK * m0 : PACK * m1])
+
         warm = keep.tile([P, 8], F32, name="warm")
         nc.vector.memset(warm[:], 0.0)
         nc.scalar.activation(out=warm[:], in_=warm[:], func=SIGMOID)
 
-        def deal(copy, g, m0, m1):
+        def deal(copy, g, raw, m0, m1):
             dst = w_bf[g][:].rearrange("p (t m j) -> p m j t", t=PACK, j=PACK)
-            src = w_raw[g][:].rearrange("p j (m t) -> p m j t", t=PACK)
-            copy(out=dst[:, m0:m1], in_=src[:, m0:m1])
+            copy(out=dst[:, m0:m1], in_=raw)
 
-        def deal_w2(copy, i):
-            m0, m1 = W2_PARTS[i]
-            dst = w_bf[2][:].rearrange("p (t m j) -> p m j t", t=PACK, j=PACK)
-            copy(out=dst[:, m0:m1], in_=w2_raw[i][:].rearrange("p j (m t) -> p m j t", t=PACK))
+        def by_slice(raw):
+            return raw[:].rearrange("p j (m t) -> p m j t", t=PACK)
 
         def quantize_w(g):
             nc.vector.quantize_mx(out=w_codes[g][:].bitcast(FP8X4), scales=w_scales[g][:], in_=w_bf[g][:])
 
         nc.vector.tensor_copy(out=x_codes[0][:], in_=x_table[0][:].indirect(offsets[:]))
-        deal(nc.scalar.copy, 0, 0, 128)
         nc.vector.tensor_copy(out=x_planes[:], in_=s_table[:].indirect(offsets[:]))
-        quantize_w(0)
-        deal(nc.scalar.copy, 1, 0, 80)
-        deal(nc.vector.tensor_copy, 1, 80, 128)
-        quantize_w(1)
+        for g in range(PASSES):
+            split = W1_SCALAR[g]
+            deal(nc.scalar.copy, g, by_slice(w1_raw[g])[:, 0:split], 0, split)
+            deal(nc.vector.tensor_copy, g, by_slice(w1_raw[g])[:, split:P], split, P)
+            quantize_w(g)
         for i in range(S // PIECE):
             nc.vector.tensor_copy(
                 out=x_codes[1][:, i * PIECE : (i + 1) * PIECE],
-                in_=x_table[1][:].indirect(offsets[:, i * PIECE // 16 : (i + 1) * PIECE // 16]),
+                in_=x_table[1][:].indirect(offsets[:, i * PIECE // LIST_ROWS : (i + 1) * PIECE // LIST_ROWS]),
             )
 
-        h_ps, h_q, gate = {}, {}, {}
+        h_ps, gate, y, y_bf = {}, {}, {}, {}
         y_rows = out_0.rearrange("(p t) n -> p t n", t=PACK)
         y_words = out_1[0].rearrange("p n t -> p (n t)").bitcast(I32)
 
+        def tokens(c):
+            return slice(c * CHUNK, (c + 1) * CHUNK)
+
+        def values(c):
+            return slice(c * CHUNK * PACK, (c + 1) * CHUNK * PACK)
+
         def first_product(c):
-            cols = slice(c * CHUNK, (c + 1) * CHUNK)
             h_ps[c] = psum_h.tile([P, PACK, CHUNK], F32, name="h")
             for t in range(PACK):
-                for g in range(2):
+                for g in range(PASSES):
                     nc.tensor.matmul_mx(
                         out=h_ps[c][:, t, :],
                         lhsT=w_codes[g][:, t * P : (t + 1) * P].bitcast(FP8X4),
                         lhsT_scale=w_scales[g][:, t * P : (t + 1) * P],
-                        rhs=x_codes[g][:, cols].bitcast(FP8X4),
-                        rhs_scale=x_planes[4 * g : P, cols],
+                        rhs=x_codes[g][:, tokens(c)].bitcast(FP8X4),
+                        rhs_scale=x_planes[SCALE_ROWS * g : P, tokens(c)],
                         start=(g == 0),
-                        stop=(g == 1),
+                        stop=(g == PASSES - 1),
                     )
 
-        y, y_bf = {}, {}
-
         def round_h(c):
-            run = h_bf[:, c * CHUNK * PACK : (c + 1) * CHUNK * PACK]
-            nc.scalar.copy(out=run.rearrange("p (n t) -> p n t", t=PACK), in_=h_ps[c][:].rearrange("p t n -> p n t"))
+            nc.scalar.copy(
+                out=h_bf[:, values(c)].rearrange("p (n t) -> p n t", t=PACK),
+                in_=h_ps[c][:].rearrange("p t n -> p n t"),
+            )
 
         def quantize_h(c):
-            cols = slice(c * CHUNK, (c + 1) * CHUNK)
-            nc.vector.quantize_mx(out=h_codes[:, cols].bitcast(FP8X4), scales=h_scales[:, cols], in_=h_bf[:, c * CHUNK * PACK : (c + 1) * CHUNK * PACK])
+            nc.vector.quantize_mx(out=h_codes[:, tokens(c)].bitcast(FP8X4), scales=h_scales[:, tokens(c)], in_=h_bf[:, values(c)])
 
         def second_product(c):
             z = psum_z.tile([P, PACK, CHUNK], F32, name="z")
-            cols = slice(c * CHUNK, (c + 1) * CHUNK)
             for t in range(PACK):
                 nc.tensor.matmul_mx(
                     out=z[:, t, :],
-                    lhsT=w_codes[2][:, t * P : (t + 1) * P].bitcast(FP8X4),
-                    lhsT_scale=w_scales[2][:, t * P : (t + 1) * P],
-                    rhs=h_codes[:, cols].bitcast(FP8X4),
-                    rhs_scale=h_scales[:, cols],
+                    lhsT=w_codes[W2][:, t * P : (t + 1) * P].bitcast(FP8X4),
+                    lhsT_scale=w_scales[W2][:, t * P : (t + 1) * P],
+                    rhs=h_codes[:, tokens(c)].bitcast(FP8X4),
+                    rhs_scale=h_scales[:, tokens(c)],
                     start=True,
                     stop=True,
                 )
@@ -144,53 +156,52 @@ def tile_picked_zgrn_lin_po_kernel(tc, x_words, x_scales, w1, w2, offs, out_0, o
             nc.scalar.activation(out=gate[c][:], in_=z[:], func=SIGMOID)
 
         def gate_h(c):
-            cols = slice(c * CHUNK, (c + 1) * CHUNK)
             y[c] = ring.tile([P, PACK, CHUNK], F32, name="y", align_bytes=64)
             nc.vector.tensor_tensor(out=y[c][:], in0=h_ps[c][:], in1=gate[c][:], op=MULT)
-            nc.sync.dma_start(out=y_rows[:, :, cols], in_=y[c][:])
+            nc.sync.dma_start(out=y_rows[:, :, tokens(c)], in_=y[c][:])
 
         def round_y(c):
             y_bf[c] = ring.tile([P, CHUNK * PACK], BF16, name="y_bf", align_bytes=64)
-            dst = y_bf[c][:].rearrange("p (c i t) -> p c t i", i=4, t=PACK)
-            src = y[c][:].rearrange("p t (c i) -> p c t i", i=4)
+            dst = y_bf[c][:].rearrange("p (run i t) -> p run t i", i=LINE, t=PACK)
+            src = y[c][:].rearrange("p t (run i) -> p run t i", i=LINE)
             if c == CHUNKS - 1:
-                nc.scalar.copy(out=dst[:, 0:12], in_=src[:, 0:12])
-                nc.vector.tensor_copy(out=dst[:, 12:32], in_=src[:, 12:32])
+                runs = CHUNK // LINE
+                nc.scalar.copy(out=dst[:, 0:LAST_SCALAR], in_=src[:, 0:LAST_SCALAR])
+                nc.vector.tensor_copy(out=dst[:, LAST_SCALAR:runs], in_=src[:, LAST_SCALAR:runs])
             elif c >= FIRST_SCALAR:
                 nc.scalar.copy(out=dst, in_=src)
             else:
                 nc.vector.tensor_copy(out=dst, in_=src)
 
         def quantize_y(c):
-            cols = slice(c * CHUNK, (c + 1) * CHUNK)
-            nc.vector.quantize_mx(out=y_codes[:, cols].bitcast(FP8X4), scales=y_scales[:, cols], in_=y_bf[c][:])
+            nc.vector.quantize_mx(out=y_codes[:, tokens(c)].bitcast(FP8X4), scales=y_scales[:, tokens(c)], in_=y_bf[c][:])
             if c % 2 == 1:
-                two = slice((c - 1) * CHUNK, (c + 1) * CHUNK)
-                nc.sync.dma_start(out=y_words[:, two], in_=y_codes[:, two].bitcast(I32))
+                pair = slice((c - 1) * CHUNK, (c + 1) * CHUNK)
+                nc.sync.dma_start(out=y_words[:, pair], in_=y_codes[:, pair].bitcast(I32))
 
-        deal_w2(nc.scalar.copy, 0)
+        deal(nc.scalar.copy, W2, by_slice(w2_raw[0]), *W2_PARTS[0])
         h_bf = keep.tile([P, S * PACK], BF16, name="h_bf", tag="w2_stage0", align_bytes=64)
-        AHEAD = 5
-        for c in range(AHEAD):
+        for c in range(H_BANKS):
             first_product(c)
             round_h(c)
-        deal_w2(nc.vector.tensor_copy, 1)
+        deal(nc.vector.tensor_copy, W2, by_slice(w2_raw[1]), *W2_PARTS[1])
         h_codes = keep.tile([P, S], U32, name="h_codes", tag="w2_stage1", align_bytes=64)
         h_scales = keep.tile([P, S], U8, name="h_scales", align_bytes=64)
         quantize_h(0)
-        quantize_w(2)
+        quantize_w(W2)
         quantize_h(1)
+
         for c in range(CHUNKS):
             second_product(c)
-            if c + 2 < CHUNKS:
-                quantize_h(c + 2)
+            if c + QUANTIZE_AHEAD < CHUNKS:
+                quantize_h(c + QUANTIZE_AHEAD)
             if c == CHUNKS - 1:
                 round_y(FIRST_SCALAR)
                 quantize_y(FIRST_SCALAR)
             gate_h(c)
-            if c + AHEAD < CHUNKS:
-                first_product(c + AHEAD)
-                round_h(c + AHEAD)
+            if c + H_BANKS < CHUNKS:
+                first_product(c + H_BANKS)
+                round_h(c + H_BANKS)
             if 0 <= c - 2 < FIRST_SCALAR:
                 quantize_y(c - 2)
             if 0 <= c - 1 < FIRST_SCALAR:
@@ -200,6 +211,10 @@ def tile_picked_zgrn_lin_po_kernel(tc, x_words, x_scales, w1, w2, offs, out_0, o
             if c > FIRST_SCALAR + 1:
                 quantize_y(c - 1)
         quantize_y(CHUNKS - 1)
-        for q in range(4):
+
+        for q in range(QUADRANTS):
             queue = nc.sync if q % 2 == 0 else nc.scalar
-            queue.dma_start(out=out_2[0, 4 * q : 4 * q + 4, :].bitcast(I32), in_=y_scales[32 * q : 32 * q + 4, :].bitcast(I32))
+            queue.dma_start(
+                out=out_2[0, SCALE_ROWS * q : SCALE_ROWS * (q + 1), :].bitcast(I32),
+                in_=y_scales[QUADRANT * q : QUADRANT * q + SCALE_ROWS, :].bitcast(I32),
+            )

@@ -117,19 +117,19 @@ def tile_picked_zgrn_lin_po_kernel(tc, x_words, x_scales, w1, w2, offs, out_0, o
         def values(c):
             return slice(c * CHUNK * PACK, (c + 1) * CHUNK * PACK)
 
-        def first_product(c):
-            h_ps[c] = psum_h.tile([P, PACK, CHUNK], F32, name="h")
+        def first_product(c, g):
+            if g == 0:
+                h_ps[c] = psum_h.tile([P, PACK, CHUNK], F32, name="h")
             for t in range(PACK):
-                for g in range(PASSES):
-                    nc.tensor.matmul_mx(
-                        out=h_ps[c][:, t, :],
-                        lhsT=w_codes[g][:, t * P : (t + 1) * P].bitcast(FP8X4),
-                        lhsT_scale=w_scales[g][:, t * P : (t + 1) * P],
-                        rhs=x_codes[g][:, tokens(c)].bitcast(FP8X4),
-                        rhs_scale=x_planes[SCALE_ROWS * g : P, tokens(c)],
-                        start=(g == 0),
-                        stop=(g == PASSES - 1),
-                    )
+                nc.tensor.matmul_mx(
+                    out=h_ps[c][:, t, :],
+                    lhsT=w_codes[g][:, t * P : (t + 1) * P].bitcast(FP8X4),
+                    lhsT_scale=w_scales[g][:, t * P : (t + 1) * P],
+                    rhs=x_codes[g][:, tokens(c)].bitcast(FP8X4),
+                    rhs_scale=x_planes[SCALE_ROWS * g : P, tokens(c)],
+                    start=(g == 0 and t == 0),
+                    stop=(g == PASSES - 1 and t == PACK - 1),
+                )
 
         def round_h(c):
             nc.scalar.copy(
@@ -182,7 +182,9 @@ def tile_picked_zgrn_lin_po_kernel(tc, x_words, x_scales, w1, w2, offs, out_0, o
         deal(nc.scalar.copy, W2, by_slice(w2_raw[0]), *W2_PARTS[0])
         h_bf = keep.tile([P, S * PACK], BF16, name="h_bf", tag="w2_stage0", align_bytes=64)
         for c in range(H_BANKS):
-            first_product(c)
+            first_product(c, 0)
+        for c in range(H_BANKS):
+            first_product(c, 1)
             round_h(c)
         deal(nc.vector.tensor_copy, W2, by_slice(w2_raw[1]), *W2_PARTS[1])
         h_codes = keep.tile([P, S], U32, name="h_codes", tag="w2_stage1", align_bytes=64)
@@ -200,7 +202,8 @@ def tile_picked_zgrn_lin_po_kernel(tc, x_words, x_scales, w1, w2, offs, out_0, o
                 quantize_y(FIRST_SCALAR)
             gate_h(c)
             if c + H_BANKS < CHUNKS:
-                first_product(c + H_BANKS)
+                for g in range(PASSES):
+                    first_product(c + H_BANKS, g)
                 round_h(c + H_BANKS)
             if 0 <= c - 2 < FIRST_SCALAR:
                 quantize_y(c - 2)

@@ -32,6 +32,7 @@ PIECE = 256
 H_BANKS = 5
 Z_BANKS = 3
 QUANTIZE_AHEAD = 2
+EARLY_PASS = 2
 
 W1_SCALAR = (96, 64)
 W2_PARTS = ((0, 64), (64, P))
@@ -117,8 +118,8 @@ def tile_picked_zgrn_lin_po_kernel(tc, x_words, x_scales, w1, w2, offs, out_0, o
         def values(c):
             return slice(c * CHUNK * PACK, (c + 1) * CHUNK * PACK)
 
-        def first_product(c, g):
-            if g == 0:
+        def first_product(c, g, opens):
+            if opens:
                 h_ps[c] = psum_h.tile([P, PACK, CHUNK], F32, name="h")
             for t in range(PACK):
                 nc.tensor.matmul_mx(
@@ -127,8 +128,8 @@ def tile_picked_zgrn_lin_po_kernel(tc, x_words, x_scales, w1, w2, offs, out_0, o
                     lhsT_scale=w_scales[g][:, t * P : (t + 1) * P],
                     rhs=x_codes[g][:, tokens(c)].bitcast(FP8X4),
                     rhs_scale=x_planes[SCALE_ROWS * g : P, tokens(c)],
-                    start=(g == 0 and t == 0),
-                    stop=(g == PASSES - 1 and t == PACK - 1),
+                    start=(opens and t == 0),
+                    stop=(not opens and t == PACK - 1),
                 )
 
         def round_h(c):
@@ -181,10 +182,12 @@ def tile_picked_zgrn_lin_po_kernel(tc, x_words, x_scales, w1, w2, offs, out_0, o
 
         deal(nc.scalar.copy, W2, by_slice(w2_raw[0]), *W2_PARTS[0])
         h_bf = keep.tile([P, S * PACK], BF16, name="h_bf", tag="w2_stage0", align_bytes=64)
+        for c in range(EARLY_PASS):
+            first_product(c, 0, True)
         for c in range(H_BANKS):
-            first_product(c, 0)
-        for c in range(H_BANKS):
-            first_product(c, 1)
+            first_product(c, 1, c >= EARLY_PASS)
+            if c >= EARLY_PASS:
+                first_product(c, 0, False)
             round_h(c)
         deal(nc.vector.tensor_copy, W2, by_slice(w2_raw[1]), *W2_PARTS[1])
         h_codes = keep.tile([P, S], U32, name="h_codes", tag="w2_stage1", align_bytes=64)
@@ -203,7 +206,7 @@ def tile_picked_zgrn_lin_po_kernel(tc, x_words, x_scales, w1, w2, offs, out_0, o
             gate_h(c)
             if c + H_BANKS < CHUNKS:
                 for g in range(PASSES):
-                    first_product(c + H_BANKS, g)
+                    first_product(c + H_BANKS, g, g == 0)
                 round_h(c + H_BANKS)
             if 0 <= c - 2 < FIRST_SCALAR:
                 quantize_y(c - 2)

@@ -26,6 +26,7 @@ SCALE_ROWS = 4
 LIST_ROWS = 16
 CHUNK = 128
 CHUNKS = S // CHUNK
+ALIGN = 256
 LINE = 4
 PIECE = 256
 
@@ -49,20 +50,20 @@ def tile_picked_zgrn_lin_po_kernel(tc, x_words, x_scales, w1, w2, offs, out_0, o
         psum_z = ctx.enter_context(tc.psum_pool(name="psum_z", bufs=Z_BANKS))
 
         offsets = keep.tile([P, S // LIST_ROWS], U16, name="offsets")
-        x_table = [keep.tile([P, T], U32, name="x_table%d" % g, align_bytes=64) for g in range(PASSES)]
-        s_table = keep.tile([P, T], U8, name="s_table", align_bytes=64)
-        w1_raw = [keep.tile([P, PACK, H], F32, name="w_raw%d" % g, tag="stage%d" % g, align_bytes=64) for g in range(PASSES)]
+        x_table = [keep.tile([P, T], U32, name="x_table%d" % g, align_bytes=ALIGN) for g in range(PASSES)]
+        s_table = keep.tile([P, T], U8, name="s_table", align_bytes=ALIGN)
+        w1_raw = [keep.tile([P, PACK, H], F32, name="w_raw%d" % g, tag="stage%d" % g, align_bytes=ALIGN) for g in range(PASSES)]
         w2_raw = [
-            keep.tile([P, PACK, PACK * (m1 - m0)], F32, name="w2_raw%d" % i, tag="w2_stage%d" % i, align_bytes=64)
+            keep.tile([P, PACK, PACK * (m1 - m0)], F32, name="w2_raw%d" % i, tag="w2_stage%d" % i, align_bytes=ALIGN)
             for i, (m0, m1) in enumerate(W2_PARTS)
         ]
-        w_bf = [keep.tile([P, PACK * H], BF16, name="w_bf%d" % g, align_bytes=64) for g in range(PASSES + 1)]
-        w_codes = [keep.tile([P, H], U32, name="w_codes%d" % g, align_bytes=64) for g in range(PASSES + 1)]
-        w_scales = [keep.tile([P, H], U8, name="w_scales%d" % g, align_bytes=64) for g in range(PASSES + 1)]
-        x_codes = [keep.tile([P, S], U32, name="x_codes%d" % g, align_bytes=64) for g in range(PASSES)]
-        x_planes = keep.tile([P, S], U8, name="x_planes", align_bytes=64)
-        y_codes = keep.tile([P, S], U32, name="y_codes", align_bytes=64)
-        y_scales = keep.tile([P, S], U8, name="y_scales", align_bytes=64)
+        w_bf = [keep.tile([P, PACK * H], BF16, name="w_bf%d" % g, align_bytes=ALIGN) for g in range(PASSES + 1)]
+        w_codes = [keep.tile([P, H], U32, name="w_codes%d" % g, align_bytes=ALIGN) for g in range(PASSES + 1)]
+        w_scales = [keep.tile([P, H], U8, name="w_scales%d" % g, align_bytes=ALIGN) for g in range(PASSES + 1)]
+        x_codes = [keep.tile([P, S], U32, name="x_codes%d" % g, align_bytes=ALIGN) for g in range(PASSES)]
+        x_planes = keep.tile([P, S], U8, name="x_planes", align_bytes=ALIGN)
+        y_codes = keep.tile([P, S], U32, name="y_codes", align_bytes=ALIGN)
+        y_scales = keep.tile([P, S], U8, name="y_scales", align_bytes=ALIGN)
 
         x_rows = [x_words[g].rearrange("p n t -> p (n t)").bitcast(I32) for g in range(PASSES)]
         nc.vector.memset(s_table[:].bitcast(I32), 0)
@@ -153,16 +154,16 @@ def tile_picked_zgrn_lin_po_kernel(tc, x_words, x_scales, w1, w2, offs, out_0, o
                     start=True,
                     stop=True,
                 )
-            gate[c] = ring.tile([P, PACK, CHUNK], F32, name="gate", align_bytes=64)
+            gate[c] = ring.tile([P, PACK, CHUNK], F32, name="gate", align_bytes=ALIGN)
             nc.scalar.activation(out=gate[c][:], in_=z[:], func=SIGMOID)
 
         def gate_h(c):
-            y[c] = ring.tile([P, PACK, CHUNK], F32, name="y", align_bytes=64)
+            y[c] = ring.tile([P, PACK, CHUNK], F32, name="y", align_bytes=ALIGN)
             nc.vector.tensor_tensor(out=y[c][:], in0=h_ps[c][:], in1=gate[c][:], op=MULT)
             nc.sync.dma_start(out=y_rows[:, :, tokens(c)], in_=y[c][:])
 
         def round_y(c):
-            y_bf[c] = ring.tile([P, CHUNK * PACK], BF16, name="y_bf", align_bytes=64)
+            y_bf[c] = ring.tile([P, CHUNK * PACK], BF16, name="y_bf", align_bytes=ALIGN)
             dst = y_bf[c][:].rearrange("p (run i t) -> p run t i", i=LINE, t=PACK)
             src = y[c][:].rearrange("p t (run i) -> p run t i", i=LINE)
             if c == CHUNKS - 1:
@@ -181,7 +182,7 @@ def tile_picked_zgrn_lin_po_kernel(tc, x_words, x_scales, w1, w2, offs, out_0, o
                 nc.sync.dma_start(out=y_words[:, pair], in_=y_codes[:, pair].bitcast(I32))
 
         deal(nc.scalar.copy, W2, by_slice(w2_raw[0]), *W2_PARTS[0])
-        h_bf = keep.tile([P, S * PACK], BF16, name="h_bf", tag="w2_stage0", align_bytes=64)
+        h_bf = keep.tile([P, S * PACK], BF16, name="h_bf", tag="w2_stage0", align_bytes=ALIGN)
         for c in range(EARLY_PASS):
             first_product(c, 0, True)
         for c in range(H_BANKS):
@@ -190,8 +191,8 @@ def tile_picked_zgrn_lin_po_kernel(tc, x_words, x_scales, w1, w2, offs, out_0, o
                 first_product(c, 0, False)
             round_h(c)
         deal(nc.vector.tensor_copy, W2, by_slice(w2_raw[1]), *W2_PARTS[1])
-        h_codes = keep.tile([P, S], U32, name="h_codes", tag="w2_stage1", align_bytes=64)
-        h_scales = keep.tile([P, S], U8, name="h_scales", align_bytes=64)
+        h_codes = keep.tile([P, S], U32, name="h_codes", tag="w2_stage1", align_bytes=ALIGN)
+        h_scales = keep.tile([P, S], U8, name="h_scales", align_bytes=ALIGN)
         quantize_h(0)
         quantize_w(W2)
         quantize_h(1)

@@ -133,14 +133,18 @@ def tile_picked_zgrn_lin_po_kernel(tc, x_words, x_scales, w1, w2, offs, out_0, o
                     stop=(not opens and t == PACK - 1),
                 )
 
+        def h_bf(c):
+            return h_bf_vector[:] if c == H_BANKS - 1 else h_bf_scalar[:, values(c)]
+
         def round_h(c):
-            nc.scalar.copy(
-                out=h_bf[:, values(c)].rearrange("p (n t) -> p n t", t=PACK),
+            copy = nc.vector.tensor_copy if c == H_BANKS - 1 else nc.scalar.copy
+            copy(
+                out=h_bf(c).rearrange("p (n t) -> p n t", t=PACK),
                 in_=h_ps[c][:].rearrange("p t n -> p n t"),
             )
 
         def quantize_h(c):
-            nc.vector.quantize_mx(out=h_codes[:, tokens(c)].bitcast(FP8X4), scales=h_scales[:, tokens(c)], in_=h_bf[:, values(c)])
+            nc.vector.quantize_mx(out=h_codes[:, tokens(c)].bitcast(FP8X4), scales=h_scales[:, tokens(c)], in_=h_bf(c))
 
         def second_product(c):
             z = psum_z.tile([P, PACK, CHUNK], F32, name="z")
@@ -182,20 +186,28 @@ def tile_picked_zgrn_lin_po_kernel(tc, x_words, x_scales, w1, w2, offs, out_0, o
                 nc.sync.dma_start(out=y_words[:, pair], in_=y_codes[:, pair].bitcast(I32))
 
         deal(nc.scalar.copy, W2, by_slice(w2_raw[0]), *W2_PARTS[0])
-        h_bf = keep.tile([P, S * PACK], BF16, name="h_bf", tag="w2_stage0", align_bytes=ALIGN)
+        h_bf_scalar = keep.tile([P, S * PACK], BF16, name="h_bf", tag="w2_stage0", align_bytes=ALIGN)
         for c in range(EARLY_PASS):
             first_product(c, 0, True)
         for c in range(H_BANKS):
             first_product(c, 1, c >= EARLY_PASS)
             if c >= EARLY_PASS:
                 first_product(c, 0, False)
-            round_h(c)
+            if c < H_BANKS - 1:
+                round_h(c)
         deal(nc.vector.tensor_copy, W2, by_slice(w2_raw[1]), *W2_PARTS[1])
-        h_codes = keep.tile([P, S], U32, name="h_codes", tag="w2_stage1", align_bytes=ALIGN)
+        h_codes = keep.tile([P, S], U32, name="h_codes", align_bytes=ALIGN)
+        h_bf_vector = keep.tile([P, CHUNK * PACK], BF16, name="h_bf_vector", tag="w2_stage1", align_bytes=ALIGN)
         h_scales = keep.tile([P, S], U8, name="h_scales", align_bytes=ALIGN)
         quantize_h(0)
-        quantize_w(W2)
+        for t in range(PACK):
+            nc.vector.quantize_mx(
+                out=w_codes[W2][:, t * P : (t + 1) * P].bitcast(FP8X4),
+                scales=w_scales[W2][:, t * P : (t + 1) * P],
+                in_=w_bf[W2][:, t * K_PASS : (t + 1) * K_PASS],
+            )
         quantize_h(1)
+        round_h(H_BANKS - 1)
 
         for c in range(CHUNKS):
             second_product(c)

@@ -32,7 +32,9 @@ PIECE = 256
 
 H_BANKS = 5
 Z_BANKS = 3
-QUANTIZE_AHEAD = 2
+TWICE = H_BANKS
+REFILL = (6, 7, TWICE)
+QUANTIZE_AHEAD = 3
 EARLY_PASS = 2
 
 W1_SCALAR = (96, 64)
@@ -46,8 +48,7 @@ def tile_picked_zgrn_lin_po_kernel(tc, x_words, x_scales, w1, w2, offs, out_0, o
     with ExitStack() as ctx:
         keep = ctx.enter_context(tc.tile_pool(name="keep", bufs=1))
         ring = ctx.enter_context(tc.tile_pool(name="ring", bufs=CHUNKS))
-        psum_h = ctx.enter_context(tc.psum_pool(name="psum_h", bufs=H_BANKS))
-        psum_z = ctx.enter_context(tc.psum_pool(name="psum_z", bufs=Z_BANKS))
+        psum = ctx.enter_context(tc.psum_pool(name="psum", bufs=1))
 
         offsets = keep.tile([P, S // LIST_ROWS], U16, name="offsets")
         x_table = [keep.tile([P, T], U32, name="x_table%d" % g, align_bytes=ALIGN) for g in range(PASSES)]
@@ -119,9 +120,12 @@ def tile_picked_zgrn_lin_po_kernel(tc, x_words, x_scales, w1, w2, offs, out_0, o
         def values(c):
             return slice(c * CHUNK * PACK, (c + 1) * CHUNK * PACK)
 
-        def first_product(c, g, opens):
+        def bank(b, name):
+            return psum.tile([P, PACK, CHUNK], F32, name=name, tag="bank%d" % b)
+
+        def first_product(c, g, opens, b):
             if opens:
-                h_ps[c] = psum_h.tile([P, PACK, CHUNK], F32, name="h")
+                h_ps[c] = bank(b, "h%d_%d" % (c, b))
             for t in range(PACK):
                 nc.tensor.matmul_mx(
                     out=h_ps[c][:, t, :],
@@ -147,7 +151,7 @@ def tile_picked_zgrn_lin_po_kernel(tc, x_words, x_scales, w1, w2, offs, out_0, o
             nc.vector.quantize_mx(out=h_codes[:, tokens(c)].bitcast(FP8X4), scales=h_scales[:, tokens(c)], in_=h_bf(c))
 
         def second_product(c):
-            z = psum_z.tile([P, PACK, CHUNK], F32, name="z")
+            z = bank(H_BANKS + c % Z_BANKS, "z%d" % c)
             for t in range(PACK):
                 nc.tensor.matmul_mx(
                     out=z[:, t, :],
@@ -188,12 +192,13 @@ def tile_picked_zgrn_lin_po_kernel(tc, x_words, x_scales, w1, w2, offs, out_0, o
         deal(nc.scalar.copy, W2, by_slice(w2_raw[0]), *W2_PARTS[0])
         h_bf_scalar = keep.tile([P, S * PACK], BF16, name="h_bf", tag="w2_stage0", align_bytes=ALIGN)
         for c in range(EARLY_PASS):
-            first_product(c, 0, True)
-        for c in range(H_BANKS):
-            first_product(c, 1, c >= EARLY_PASS)
+            first_product(c, 0, True, c)
+        for c in range(TWICE + 1):
+            b = H_BANKS + Z_BANKS - 1 if c == TWICE else c
+            first_product(c, 1, c >= EARLY_PASS, b)
             if c >= EARLY_PASS:
-                first_product(c, 0, False)
-            if c < H_BANKS - 1:
+                first_product(c, 0, False, b)
+            if c != H_BANKS - 1:
                 round_h(c)
         deal(nc.vector.tensor_copy, W2, by_slice(w2_raw[1]), *W2_PARTS[1])
         h_codes = keep.tile([P, S], U32, name="h_codes", align_bytes=ALIGN)
@@ -208,6 +213,7 @@ def tile_picked_zgrn_lin_po_kernel(tc, x_words, x_scales, w1, w2, offs, out_0, o
             )
         quantize_h(1)
         round_h(H_BANKS - 1)
+        quantize_h(2)
 
         for c in range(CHUNKS):
             second_product(c)
@@ -217,10 +223,11 @@ def tile_picked_zgrn_lin_po_kernel(tc, x_words, x_scales, w1, w2, offs, out_0, o
                 round_y(FIRST_SCALAR)
                 quantize_y(FIRST_SCALAR)
             gate_h(c)
-            if c + H_BANKS < CHUNKS:
+            if c < len(REFILL):
                 for g in range(PASSES):
-                    first_product(c + H_BANKS, g, g == 0)
-                round_h(c + H_BANKS)
+                    first_product(REFILL[c], g, g == 0, c)
+                if REFILL[c] != TWICE:
+                    round_h(REFILL[c])
             if 0 <= c - 2 < FIRST_SCALAR:
                 quantize_y(c - 2)
             if 0 <= c - 1 < FIRST_SCALAR:

@@ -14,6 +14,7 @@ U8 = mybir.dt.uint8
 FP8X4 = mybir.dt.float8_e4m3fn_x4
 SIGMOID = mybir.ActivationFunctionType.Sigmoid
 MULT = mybir.AluOpType.mult
+ADD = mybir.AluOpType.add
 
 P = 128
 PACK = 4
@@ -38,7 +39,7 @@ QUANTIZE_AHEAD = 3
 EARLY_PASS = 2
 
 W1_SCALAR = (96, 64)
-W2_PARTS = ((0, 64), (64, P))
+W2_PARTS = ((0, 48), (48, P))
 FIRST_SCALAR = 4
 LAST_SCALAR = 12
 
@@ -58,7 +59,7 @@ def tile_picked_zgrn_lin_po_kernel(tc, x_words, x_scales, w1, w2, offs, out_0, o
             keep.tile([P, PACK, PACK * (m1 - m0)], F32, name="w2_raw%d" % i, tag="w2_stage%d" % i, align_bytes=ALIGN)
             for i, (m0, m1) in enumerate(W2_PARTS)
         ]
-        w_bf = [keep.tile([P, PACK * H], BF16, name="w_bf%d" % g, align_bytes=ALIGN) for g in range(PASSES + 1)]
+        w_bf = [keep.tile([P, PACK * H], BF16, name="w_bf%d" % g, tag="w_bf%d" % g, align_bytes=ALIGN) for g in range(PASSES + 1)]
         w_codes = [keep.tile([P, H], U32, name="w_codes%d" % g, align_bytes=ALIGN) for g in range(PASSES + 1)]
         w_scales = [keep.tile([P, H], U8, name="w_scales%d" % g, align_bytes=ALIGN) for g in range(PASSES + 1)]
         x_codes = [keep.tile([P, S], U32, name="x_codes%d" % g, align_bytes=ALIGN) for g in range(PASSES)]
@@ -88,8 +89,13 @@ def tile_picked_zgrn_lin_po_kernel(tc, x_words, x_scales, w1, w2, offs, out_0, o
         nc.scalar.activation(out=warm[:], in_=warm[:], func=SIGMOID)
 
         def deal(copy, g, raw, m0, m1):
-            dst = w_bf[g][:].rearrange("p (t m j) -> p m j t", t=PACK, j=PACK)
-            copy(out=dst[:, m0:m1], in_=raw)
+            dst = w_bf[g][:].rearrange("p (t m j) -> p m j t", t=PACK, j=PACK)[:, m0:m1]
+            walk = "p (pair e) j t -> p pair j e t"
+            copy(out=dst.rearrange(walk, e=2), in_=raw.rearrange(walk, e=2))
+
+        def gpsimd_copy(out, in_):
+            walk = "p pair j e t -> p t pair e j"
+            nc.gpsimd.tensor_scalar(out=out.rearrange(walk), in0=in_.rearrange(walk), scalar1=1.0, scalar2=0.0, op0=MULT, op1=ADD)
 
         def by_slice(raw):
             return raw[:].rearrange("p j (m t) -> p m j t", t=PACK)
@@ -138,10 +144,10 @@ def tile_picked_zgrn_lin_po_kernel(tc, x_words, x_scales, w1, w2, offs, out_0, o
                 )
 
         def h_bf(c):
-            return h_bf_vector[:] if c == H_BANKS - 1 else h_bf_scalar[:, values(c)]
+            return h_bf_vector[:] if c == TWICE else h_bf_scalar[:, values(c)]
 
         def round_h(c):
-            copy = nc.vector.tensor_copy if c == H_BANKS - 1 else nc.scalar.copy
+            copy = nc.vector.tensor_copy if c == TWICE else nc.scalar.copy
             copy(
                 out=h_bf(c).rearrange("p (n t) -> p n t", t=PACK),
                 in_=h_ps[c][:].rearrange("p t n -> p n t"),
@@ -178,7 +184,7 @@ def tile_picked_zgrn_lin_po_kernel(tc, x_words, x_scales, w1, w2, offs, out_0, o
                 runs = CHUNK // LINE
                 nc.scalar.copy(out=dst[:, 0:LAST_SCALAR], in_=src[:, 0:LAST_SCALAR])
                 nc.vector.tensor_copy(out=dst[:, LAST_SCALAR:runs], in_=src[:, LAST_SCALAR:runs])
-            elif c >= FIRST_SCALAR:
+            elif c >= FIRST_SCALAR or c == 0:
                 nc.scalar.copy(out=dst, in_=src)
             else:
                 nc.vector.tensor_copy(out=dst, in_=src)
@@ -189,8 +195,8 @@ def tile_picked_zgrn_lin_po_kernel(tc, x_words, x_scales, w1, w2, offs, out_0, o
                 pair = slice((c - 1) * CHUNK, (c + 1) * CHUNK)
                 nc.sync.dma_start(out=y_words[:, pair], in_=y_codes[:, pair].bitcast(I32))
 
-        deal(nc.scalar.copy, W2, by_slice(w2_raw[0]), *W2_PARTS[0])
-        h_bf_scalar = keep.tile([P, S * PACK], BF16, name="h_bf", tag="w2_stage0", align_bytes=ALIGN)
+        deal(gpsimd_copy, W2, by_slice(w2_raw[0]), *W2_PARTS[0])
+        h_bf_scalar = keep.tile([P, S * PACK], BF16, name="h_bf", align_bytes=ALIGN)
         for c in range(EARLY_PASS):
             first_product(c, 0, True, c)
         for c in range(TWICE + 1):
@@ -198,11 +204,10 @@ def tile_picked_zgrn_lin_po_kernel(tc, x_words, x_scales, w1, w2, offs, out_0, o
             first_product(c, 1, c >= EARLY_PASS, b)
             if c >= EARLY_PASS:
                 first_product(c, 0, False, b)
-            if c != H_BANKS - 1:
+            if c != TWICE:
                 round_h(c)
         deal(nc.vector.tensor_copy, W2, by_slice(w2_raw[1]), *W2_PARTS[1])
-        h_codes = keep.tile([P, S], U32, name="h_codes", align_bytes=ALIGN)
-        h_bf_vector = keep.tile([P, CHUNK * PACK], BF16, name="h_bf_vector", tag="w2_stage1", align_bytes=ALIGN)
+        h_codes = keep.tile([P, S], U32, name="h_codes", tag="w2_stage1", align_bytes=ALIGN)
         h_scales = keep.tile([P, S], U8, name="h_scales", align_bytes=ALIGN)
         quantize_h(0)
         for t in range(PACK):
@@ -212,7 +217,8 @@ def tile_picked_zgrn_lin_po_kernel(tc, x_words, x_scales, w1, w2, offs, out_0, o
                 in_=w_bf[W2][:, t * K_PASS : (t + 1) * K_PASS],
             )
         quantize_h(1)
-        round_h(H_BANKS - 1)
+        h_bf_vector = keep.tile([P, CHUNK * PACK], BF16, name="h_bf_vector", tag="w_bf%d" % W2, align_bytes=ALIGN)
+        round_h(TWICE)
         quantize_h(2)
 
         for c in range(CHUNKS):

@@ -29,19 +29,19 @@ CHUNK = 128
 CHUNKS = S // CHUNK
 ALIGN = 256
 LINE = 4
-PIECE = 256
+PIECES = ((0, 128), (128, 384), (384, 768), (768, 1024))
 
 H_BANKS = 5
 Z_BANKS = 3
-TWICE = H_BANKS
-REFILL = (6, 7, TWICE)
-QUANTIZE_AHEAD = 3
-EARLY_PASS = 2
+TWICE = (5, 6)
+LAST = CHUNKS - 1
+REFILL = (LAST,) + TWICE
+H_VECTOR = TWICE[0]
+EARLY_PASS = 4
 
 W1_SCALAR = (96, 64)
 W2_PARTS = ((0, 48), (48, P))
-FIRST_SCALAR = 4
-LAST_SCALAR = 12
+RUN = 4
 
 
 def tile_picked_zgrn_lin_po_kernel(tc, x_words, x_scales, w1, w2, offs, out_0, out_1, out_2):
@@ -64,7 +64,6 @@ def tile_picked_zgrn_lin_po_kernel(tc, x_words, x_scales, w1, w2, offs, out_0, o
         w_scales = [keep.tile([P, H], U8, name="w_scales%d" % g, align_bytes=ALIGN) for g in range(PASSES + 1)]
         x_codes = [keep.tile([P, S], U32, name="x_codes%d" % g, align_bytes=ALIGN) for g in range(PASSES)]
         x_planes = keep.tile([P, S], U8, name="x_planes", align_bytes=ALIGN)
-        y_codes = keep.tile([P, S], U32, name="y_codes", align_bytes=ALIGN)
         y_scales = keep.tile([P, S], U8, name="y_scales", align_bytes=ALIGN)
 
         x_rows = [x_words[g].rearrange("p n t -> p (n t)").bitcast(I32) for g in range(PASSES)]
@@ -94,8 +93,11 @@ def tile_picked_zgrn_lin_po_kernel(tc, x_words, x_scales, w1, w2, offs, out_0, o
             copy(out=dst.rearrange(walk, e=2), in_=raw.rearrange(walk, e=2))
 
         def gpsimd_copy(out, in_):
+            nc.gpsimd.tensor_scalar(out=out, in0=in_, scalar1=1.0, scalar2=0.0, op0=MULT, op1=ADD)
+
+        def gpsimd_deal(out, in_):
             walk = "p pair j e t -> p t pair e j"
-            nc.gpsimd.tensor_scalar(out=out.rearrange(walk), in0=in_.rearrange(walk), scalar1=1.0, scalar2=0.0, op0=MULT, op1=ADD)
+            gpsimd_copy(out.rearrange(walk), in_.rearrange(walk))
 
         def by_slice(raw):
             return raw[:].rearrange("p j (m t) -> p m j t", t=PACK)
@@ -110,13 +112,12 @@ def tile_picked_zgrn_lin_po_kernel(tc, x_words, x_scales, w1, w2, offs, out_0, o
             deal(nc.scalar.copy, g, by_slice(w1_raw[g])[:, 0:split], 0, split)
             deal(nc.vector.tensor_copy, g, by_slice(w1_raw[g])[:, split:P], split, P)
             quantize_w(g)
-        for i in range(S // PIECE):
+        for e0, e1 in PIECES:
             nc.vector.tensor_copy(
-                out=x_codes[1][:, i * PIECE : (i + 1) * PIECE],
-                in_=x_table[1][:].indirect(offsets[:, i * PIECE // LIST_ROWS : (i + 1) * PIECE // LIST_ROWS]),
+                out=x_codes[1][:, e0:e1], in_=x_table[1][:].indirect(offsets[:, e0 // LIST_ROWS : e1 // LIST_ROWS])
             )
 
-        h_ps, gate, y, y_bf = {}, {}, {}, {}
+        h_ps, z_ps, gate, y = {}, {}, {}, {}
         y_rows = out_0.rearrange("(p t) n -> p t n", t=PACK)
         y_words = out_1[0].rearrange("p n t -> p (n t)").bitcast(I32)
 
@@ -144,10 +145,10 @@ def tile_picked_zgrn_lin_po_kernel(tc, x_words, x_scales, w1, w2, offs, out_0, o
                 )
 
         def h_bf(c):
-            return h_bf_vector[:] if c == TWICE else h_bf_scalar[:, values(c)]
+            return h_bf_vector[:] if c == H_VECTOR else h_bf_scalar[:, values(c)]
 
         def round_h(c):
-            copy = nc.vector.tensor_copy if c == TWICE else nc.scalar.copy
+            copy = nc.vector.tensor_copy if c == H_VECTOR else nc.scalar.copy
             copy(
                 out=h_bf(c).rearrange("p (n t) -> p n t", t=PACK),
                 in_=h_ps[c][:].rearrange("p t n -> p n t"),
@@ -168,43 +169,46 @@ def tile_picked_zgrn_lin_po_kernel(tc, x_words, x_scales, w1, w2, offs, out_0, o
                     start=True,
                     stop=True,
                 )
-            gate[c] = ring.tile([P, PACK, CHUNK], F32, name="gate", align_bytes=ALIGN)
-            nc.scalar.activation(out=gate[c][:], in_=z[:], func=SIGMOID)
+            z_ps[c] = z
+
+        def sigmoid(c):
+            gate[c] = keep.tile([P, PACK, CHUNK], F32, name="gate%d" % c, tag="gate%d" % c, align_bytes=ALIGN)
+            nc.scalar.activation(out=gate[c][:], in_=z_ps[c][:], func=SIGMOID)
+
+        def refill(i):
+            for g in range(PASSES):
+                first_product(REFILL[i], g, g == 0, i)
 
         def gate_h(c):
             y[c] = ring.tile([P, PACK, CHUNK], F32, name="y", align_bytes=ALIGN)
             nc.vector.tensor_tensor(out=y[c][:], in0=h_ps[c][:], in1=gate[c][:], op=MULT)
             nc.sync.dma_start(out=y_rows[:, :, tokens(c)], in_=y[c][:])
 
-        def round_y(c):
-            y_bf[c] = ring.tile([P, CHUNK * PACK], BF16, name="y_bf", align_bytes=ALIGN)
-            dst = y_bf[c][:].rearrange("p (run i t) -> p run t i", i=LINE, t=PACK)
-            src = y[c][:].rearrange("p t (run i) -> p run t i", i=LINE)
-            if c == CHUNKS - 1:
-                runs = CHUNK // LINE
-                nc.scalar.copy(out=dst[:, 0:LAST_SCALAR], in_=src[:, 0:LAST_SCALAR])
-                nc.vector.tensor_copy(out=dst[:, LAST_SCALAR:runs], in_=src[:, LAST_SCALAR:runs])
-            elif c >= FIRST_SCALAR or c == 0:
-                nc.scalar.copy(out=dst, in_=src)
-            else:
-                nc.vector.tensor_copy(out=dst, in_=src)
+        def round_y(c, dst, copy):
+            copy(
+                out=dst.rearrange("p (run i t) -> p run t i", i=LINE, t=PACK),
+                in_=y[c][:].rearrange("p t (run i) -> p run t i", i=LINE),
+            )
 
-        def quantize_y(c):
-            nc.vector.quantize_mx(out=y_codes[:, tokens(c)].bitcast(FP8X4), scales=y_scales[:, tokens(c)], in_=y_bf[c][:])
-            if c % 2 == 1:
-                pair = slice((c - 1) * CHUNK, (c + 1) * CHUNK)
-                nc.sync.dma_start(out=y_words[:, pair], in_=y_codes[:, pair].bitcast(I32))
+        def round_y_gpsimd(c, dst):
+            gpsimd_copy(dst.rearrange("p (n t) -> p n t", t=PACK), y[c][:].rearrange("p t n -> p n t"))
 
-        deal(gpsimd_copy, W2, by_slice(w2_raw[0]), *W2_PARTS[0])
+        def quantize_y(c0, c1, codes, src):
+            nc.vector.quantize_mx(out=codes.bitcast(FP8X4), scales=y_scales[:, c0 * CHUNK : c1 * CHUNK], in_=src)
+
+        def store_codes(c0, c1, codes):
+            nc.sync.dma_start(out=y_words[:, c0 * CHUNK : c1 * CHUNK], in_=codes.bitcast(I32))
+
+        deal(gpsimd_deal, W2, by_slice(w2_raw[0]), *W2_PARTS[0])
         h_bf_scalar = keep.tile([P, S * PACK], BF16, name="h_bf", align_bytes=ALIGN)
         for c in range(EARLY_PASS):
             first_product(c, 0, True, c)
-        for c in range(TWICE + 1):
-            b = H_BANKS + Z_BANKS - 1 if c == TWICE else c
+        for c in range(LAST):
+            b = c + 1 if c in TWICE else c
             first_product(c, 1, c >= EARLY_PASS, b)
             if c >= EARLY_PASS:
                 first_product(c, 0, False, b)
-            if c != TWICE:
+            if c != H_VECTOR:
                 round_h(c)
         deal(nc.vector.tensor_copy, W2, by_slice(w2_raw[1]), *W2_PARTS[1])
         h_codes = keep.tile([P, S], U32, name="h_codes", tag="w2_stage1", align_bytes=ALIGN)
@@ -218,31 +222,53 @@ def tile_picked_zgrn_lin_po_kernel(tc, x_words, x_scales, w1, w2, offs, out_0, o
             )
         quantize_h(1)
         h_bf_vector = keep.tile([P, CHUNK * PACK], BF16, name="h_bf_vector", tag="w_bf%d" % W2, align_bytes=ALIGN)
-        round_h(TWICE)
-        quantize_h(2)
+        round_h(H_VECTOR)
+        for c in range(2, LAST):
+            quantize_h(c)
 
-        for c in range(CHUNKS):
+        def pair(name, tag, dtype, columns):
+            return keep.tile([P, 2 * columns], dtype, name=name, tag=tag, align_bytes=ALIGN)
+
+        def finish(c, tag, src):
+            codes = pair("y_codes%d" % c, tag, U32, CHUNK)
+            quantize_y(c, c + 2, codes[:], src[:])
+            store_codes(c, c + 2, codes[:])
+
+        y_bf01 = pair("y_bf01", "y_bf_gpsimd", BF16, CHUNK * PACK)
+        for c in range(RUN):
             second_product(c)
-            if c + QUANTIZE_AHEAD < CHUNKS:
-                quantize_h(c + QUANTIZE_AHEAD)
-            if c == CHUNKS - 1:
-                round_y(FIRST_SCALAR)
-                quantize_y(FIRST_SCALAR)
+            sigmoid(c)
+        for c in range(RUN):
             gate_h(c)
-            if c < len(REFILL):
-                for g in range(PASSES):
-                    first_product(REFILL[c], g, g == 0, c)
-                if REFILL[c] != TWICE:
-                    round_h(REFILL[c])
-            if 0 <= c - 2 < FIRST_SCALAR:
-                quantize_y(c - 2)
-            if 0 <= c - 1 < FIRST_SCALAR:
-                round_y(c - 1)
-        for c in range(FIRST_SCALAR + 1, CHUNKS):
-            round_y(c)
-            if c > FIRST_SCALAR + 1:
-                quantize_y(c - 1)
-        quantize_y(CHUNKS - 1)
+            if c < 2:
+                round_y_gpsimd(c, y_bf01[:, values(c)])
+        refill(0)
+        for c in range(RUN, LAST):
+            second_product(c)
+        refill(1)
+        refill(2)
+        round_h(LAST)
+        quantize_h(LAST)
+        finish(0, "gate%d" % (RUN - 1), y_bf01)
+
+        y_bf23 = pair("y_bf23", "y_bf_gpsimd", BF16, CHUNK * PACK)
+        for c in range(RUN, CHUNKS):
+            if c == LAST:
+                second_product(c)
+            sigmoid(c)
+        for c in range(RUN, CHUNKS):
+            gate_h(c)
+        for c in (2, 3):
+            round_y_gpsimd(c, y_bf23[:, values(c - 2)])
+        y_bf45 = pair("y_bf45", "w2_stage1", BF16, CHUNK * PACK)
+        y_bf67 = pair("y_bf67", "y_bf67", BF16, CHUNK * PACK)
+        for c in (4, 5):
+            round_y(c, y_bf45[:, values(c - 4)], nc.scalar.copy)
+        round_y(6, y_bf67[:, values(0)], nc.scalar.copy)
+        finish(2, "gate%d" % LAST, y_bf23)
+        round_y(LAST, y_bf67[:, values(1)], nc.vector.tensor_copy)
+        finish(4, "y_codes4", y_bf45)
+        finish(6, "y_codes6", y_bf67)
 
         for q in range(QUADRANTS):
             queue = nc.sync if q % 2 == 0 else nc.scalar

@@ -39,7 +39,8 @@ REFILL = (LAST,) + TWICE
 H_VECTOR = TWICE[0]
 EARLY_PASS = 4
 
-W1_SCALAR = (96, 64)
+EARLY_MOVES = 5
+W1_SCALAR = (56, 44)
 W2_PARTS = ((0, 48), (48, P))
 RUN = 4
 
@@ -52,36 +53,53 @@ def tile_picked_zgrn_lin_po_kernel(tc, x_words, x_scales, w1, w2, offs, out_0, o
         psum = ctx.enter_context(tc.psum_pool(name="psum", bufs=1))
 
         offsets = keep.tile([P, S // LIST_ROWS], U16, name="offsets")
-        x_table = [keep.tile([P, T], U32, name="x_table%d" % g, align_bytes=ALIGN) for g in range(PASSES)]
-        s_table = keep.tile([P, T], U8, name="s_table", align_bytes=ALIGN)
+        x_table = [keep.tile([P, T], U32, name="x_table0", tag="first", align_bytes=ALIGN)]
+        s_table = keep.tile([P, T], U8, name="s_table", tag="second", align_bytes=ALIGN)
+        s_picked = keep.tile([P, S], U8, name="s_picked", align_bytes=ALIGN)
         w1_raw = [keep.tile([P, PACK, H], F32, name="w_raw%d" % g, tag="stage%d" % g, align_bytes=ALIGN) for g in range(PASSES)]
-        w2_raw = [
-            keep.tile([P, PACK, PACK * (m1 - m0)], F32, name="w2_raw%d" % i, tag="w2_stage%d" % i, align_bytes=ALIGN)
-            for i, (m0, m1) in enumerate(W2_PARTS)
-        ]
         w_bf = [keep.tile([P, PACK * H], BF16, name="w_bf%d" % g, tag="w_bf%d" % g, align_bytes=ALIGN) for g in range(PASSES + 1)]
         w_codes = [keep.tile([P, H], U32, name="w_codes%d" % g, align_bytes=ALIGN) for g in range(PASSES + 1)]
         w_scales = [keep.tile([P, H], U8, name="w_scales%d" % g, align_bytes=ALIGN) for g in range(PASSES + 1)]
         x_codes = [keep.tile([P, S], U32, name="x_codes%d" % g, align_bytes=ALIGN) for g in range(PASSES)]
-        x_planes = keep.tile([P, S], U8, name="x_planes", align_bytes=ALIGN)
+        x_planes = [keep.tile([P, S], U8, name="x_planes%d" % g, align_bytes=ALIGN) for g in range(PASSES)]
         y_scales = keep.tile([P, S], U8, name="y_scales", align_bytes=ALIGN)
 
         x_rows = [x_words[g].rearrange("p n t -> p (n t)").bitcast(I32) for g in range(PASSES)]
-        nc.vector.memset(s_table[:].bitcast(I32), 0)
-        for half in range(2):
-            cols = slice(half * T // 2, (half + 1) * T // 2)
-            nc.sync.dma_start(out=x_table[0][:, cols].bitcast(I32), in_=x_rows[0][:, cols])
+        nc.vector.memset(s_table[0 : P - QUADRANT, :].bitcast(I32), 0)
+        for g in range(PASSES):
+            nc.gpsimd.memset(x_planes[g][:].bitcast(I32), 0)
+        nc.sync.dma_start(
+            out=s_table[P - QUADRANT : P, :].bitcast(I32), in_=x_scales.rearrange("g r n -> (g r) n").bitcast(I32)
+        )
         nc.sync.dma_start(offsets[:], offs)
-        for q in range(QUADRANTS):
-            nc.sync.dma_start(
-                out=s_table[QUADRANT * q : QUADRANT * q + PASSES * SCALE_ROWS, :].bitcast(I32),
-                in_=x_scales[:, SCALE_ROWS * q : SCALE_ROWS * (q + 1), :].bitcast(I32),
-            )
+        nc.sync.dma_start(out=x_table[0][:].bitcast(I32), in_=x_rows[0])
         for g in range(PASSES):
             nc.sync.dma_start(out=w1_raw[g][:], in_=w1[g * K_PASS : (g + 1) * K_PASS, :].rearrange("(p j) c -> p j c", j=PACK))
+
+        nc.vector.tensor_copy(out=s_picked[:], in_=s_table[:].indirect(offsets[:]))
+
+        def place_rows(g, q):
+            src = P - QUADRANT + SCALE_ROWS * (QUADRANTS * g + q)
+            dst = QUADRANT * q + SCALE_ROWS * g
+            nc.sync.dma_start(
+                out=x_planes[g][dst : dst + SCALE_ROWS, :].bitcast(I32), in_=s_picked[src : src + SCALE_ROWS, :].bitcast(I32)
+            )
+
+        moves = [(g, q) for g in range(PASSES) for q in range(QUADRANTS)]
+        for g, q in moves[:EARLY_MOVES]:
+            place_rows(g, q)
+        x_table.append(keep.tile([P, T], U32, name="x_table1", tag="second", align_bytes=ALIGN))
         nc.sync.dma_start(out=x_table[1][:].bitcast(I32), in_=x_rows[1])
+        for g, q in moves[EARLY_MOVES:]:
+            place_rows(g, q)
+
+        nc.vector.tensor_copy(out=x_codes[0][:], in_=x_table[0][:].indirect(offsets[:]))
+        w2_stage = keep.tile([P, PACK * H], F32, name="w2_stage", tag="first", align_bytes=ALIGN)
+        w2_raw = [
+            w2_stage[:, PACK * PACK * m0 : PACK * PACK * m1].rearrange("p (j c) -> p j c", j=PACK) for m0, m1 in W2_PARTS
+        ]
         for i, (m0, m1) in enumerate(W2_PARTS):
-            nc.sync.dma_start(out=w2_raw[i][:], in_=w2.rearrange("(p j) c -> p j c", j=PACK)[:, :, PACK * m0 : PACK * m1])
+            nc.sync.dma_start(out=w2_raw[i], in_=w2.rearrange("(p j) c -> p j c", j=PACK)[:, :, PACK * m0 : PACK * m1])
 
         warm = keep.tile([P, 8], F32, name="warm")
         nc.vector.memset(warm[:], 0.0)
@@ -100,17 +118,15 @@ def tile_picked_zgrn_lin_po_kernel(tc, x_words, x_scales, w1, w2, offs, out_0, o
             gpsimd_copy(out.rearrange(walk), in_.rearrange(walk))
 
         def by_slice(raw):
-            return raw[:].rearrange("p j (m t) -> p m j t", t=PACK)
+            return raw.rearrange("p j (m t) -> p m j t", t=PACK)
 
         def quantize_w(g):
             nc.vector.quantize_mx(out=w_codes[g][:].bitcast(FP8X4), scales=w_scales[g][:], in_=w_bf[g][:])
 
-        nc.vector.tensor_copy(out=x_codes[0][:], in_=x_table[0][:].indirect(offsets[:]))
-        nc.vector.tensor_copy(out=x_planes[:], in_=s_table[:].indirect(offsets[:]))
         for g in range(PASSES):
             split = W1_SCALAR[g]
-            deal(nc.scalar.copy, g, by_slice(w1_raw[g])[:, 0:split], 0, split)
-            deal(nc.vector.tensor_copy, g, by_slice(w1_raw[g])[:, split:P], split, P)
+            deal(nc.scalar.copy, g, by_slice(w1_raw[g][:])[:, 0:split], 0, split)
+            deal(nc.vector.tensor_copy, g, by_slice(w1_raw[g][:])[:, split:P], split, P)
             quantize_w(g)
         for e0, e1 in PIECES:
             nc.vector.tensor_copy(
@@ -139,7 +155,7 @@ def tile_picked_zgrn_lin_po_kernel(tc, x_words, x_scales, w1, w2, offs, out_0, o
                     lhsT=w_codes[g][:, t * P : (t + 1) * P].bitcast(FP8X4),
                     lhsT_scale=w_scales[g][:, t * P : (t + 1) * P],
                     rhs=x_codes[g][:, tokens(c)].bitcast(FP8X4),
-                    rhs_scale=x_planes[SCALE_ROWS * g : P, tokens(c)],
+                    rhs_scale=x_planes[g][SCALE_ROWS * g : P, tokens(c)],
                     start=(opens and t == 0),
                     stop=(not opens and t == PACK - 1),
                 )
@@ -211,7 +227,7 @@ def tile_picked_zgrn_lin_po_kernel(tc, x_words, x_scales, w1, w2, offs, out_0, o
             if c != H_VECTOR:
                 round_h(c)
         deal(nc.vector.tensor_copy, W2, by_slice(w2_raw[1]), *W2_PARTS[1])
-        h_codes = keep.tile([P, S], U32, name="h_codes", tag="w2_stage1", align_bytes=ALIGN)
+        h_codes = keep.tile([P, S], U32, name="h_codes", tag="first", align_bytes=ALIGN)
         h_scales = keep.tile([P, S], U8, name="h_scales", align_bytes=ALIGN)
         quantize_h(0)
         for t in range(PACK):
@@ -260,7 +276,7 @@ def tile_picked_zgrn_lin_po_kernel(tc, x_words, x_scales, w1, w2, offs, out_0, o
             gate_h(c)
         for c in (2, 3):
             round_y_gpsimd(c, y_bf23[:, values(c - 2)])
-        y_bf45 = pair("y_bf45", "w2_stage1", BF16, CHUNK * PACK)
+        y_bf45 = pair("y_bf45", "first", BF16, CHUNK * PACK)
         y_bf67 = pair("y_bf67", "y_bf67", BF16, CHUNK * PACK)
         for c in (4, 5):
             round_y(c, y_bf45[:, values(c - 4)], nc.scalar.copy)

@@ -105,10 +105,10 @@ def tile_picked_zgrn_lin_po_kernel(tc, x_words, x_scales, w1, w2, offs, out_0, o
         nc.vector.memset(warm[:], 0.0)
         nc.scalar.activation(out=warm[:], in_=warm[:], func=SIGMOID)
 
-        def deal(copy, g, raw, m0, m1):
-            dst = w_bf[g][:].rearrange("p (t m j) -> p m j t", t=PACK, j=PACK)[:, m0:m1]
+        def deal(copy, g, raw, m0, m1, t0=0, t1=PACK):
+            dst = w_bf[g][:].rearrange("p (t m j) -> p m j t", t=PACK, j=PACK)[:, m0:m1, :, t0:t1]
             walk = "p (pair e) j t -> p pair j e t"
-            copy(out=dst.rearrange(walk, e=2), in_=raw.rearrange(walk, e=2))
+            copy(out=dst.rearrange(walk, e=2), in_=raw[:, :, :, t0:t1].rearrange(walk, e=2))
 
         def gpsimd_copy(out, in_):
             nc.gpsimd.tensor_scalar(out=out, in0=in_, scalar1=1.0, scalar2=0.0, op0=MULT, op1=ADD)
@@ -226,11 +226,13 @@ def tile_picked_zgrn_lin_po_kernel(tc, x_words, x_scales, w1, w2, offs, out_0, o
                 first_product(c, 0, False, b)
             if c != H_VECTOR:
                 round_h(c)
-        deal(nc.vector.tensor_copy, W2, by_slice(w2_raw[1]), *W2_PARTS[1])
+        for t in range(0, PACK, 2):
+            deal(nc.vector.tensor_copy, W2, by_slice(w2_raw[1]), *W2_PARTS[1], t, t + 2)
         h_codes = keep.tile([P, S], U32, name="h_codes", tag="first", align_bytes=ALIGN)
         h_scales = keep.tile([P, S], U8, name="h_scales", align_bytes=ALIGN)
-        quantize_h(0)
         for t in range(PACK):
+            if t == 2:
+                quantize_h(0)
             nc.vector.quantize_mx(
                 out=w_codes[W2][:, t * P : (t + 1) * P].bitcast(FP8X4),
                 scales=w_scales[W2][:, t * P : (t + 1) * P],

@@ -120,14 +120,20 @@ def tile_picked_zgrn_lin_po_kernel(tc, x_words, x_scales, w1, w2, offs, out_0, o
         def by_slice(raw):
             return raw.rearrange("p j (m t) -> p m j t", t=PACK)
 
-        def quantize_w(g):
-            nc.vector.quantize_mx(out=w_codes[g][:].bitcast(FP8X4), scales=w_scales[g][:], in_=w_bf[g][:])
+        def quantize_w(g, t0, t1):
+            nc.vector.quantize_mx(
+                out=w_codes[g][:, t0 * P : t1 * P].bitcast(FP8X4),
+                scales=w_scales[g][:, t0 * P : t1 * P],
+                in_=w_bf[g][:, t0 * K_PASS : t1 * K_PASS],
+            )
 
         for g in range(PASSES):
             split = W1_SCALAR[g]
-            deal(nc.scalar.copy, g, by_slice(w1_raw[g][:])[:, 0:split], 0, split)
-            deal(nc.vector.tensor_copy, g, by_slice(w1_raw[g][:])[:, split:P], split, P)
-            quantize_w(g)
+            for t in range(0, PACK, 2):
+                deal(nc.scalar.copy, g, by_slice(w1_raw[g][:])[:, 0:split], 0, split, t, t + 2)
+                deal(nc.vector.tensor_copy, g, by_slice(w1_raw[g][:])[:, split:P], split, P, t, t + 2)
+            for t in range(0, PACK, 2):
+                quantize_w(g, t, t + 2)
         for e0, e1 in PIECES:
             nc.vector.tensor_copy(
                 out=x_codes[1][:, e0:e1], in_=x_table[1][:].indirect(offsets[:, e0 // LIST_ROWS : e1 // LIST_ROWS])

from contextlib import ExitStack

import concourse.mybir as mybir

K, T, S, H = 1024, 2048, 1024, 512
FLOPS = 2 * K * H * S + 2 * H * H * S

F32 = mybir.dt.float32
BF16 = mybir.dt.bfloat16
I32 = mybir.dt.int32
U32 = mybir.dt.uint32
U16 = mybir.dt.uint16
U8 = mybir.dt.uint8
FP8X4 = mybir.dt.float8_e4m3fn_x4
SIGMOID = mybir.ActivationFunctionType.Sigmoid
MULT = mybir.AluOpType.mult
ADD = mybir.AluOpType.add

P = 128
PACK = 4
K_PASS = P * PACK
PASSES = K // K_PASS
W2 = PASSES
QUADRANTS = 4
QUADRANT = P // QUADRANTS
SCALE_ROWS = 4
LIST_ROWS = 16
CHUNK = 128
CHUNKS = S // CHUNK
ALIGN = 256
LINE = 4
PIECES = ((0, 128), (128, 384), (384, 768), (768, 1024))

H_BANKS = 5
Z_BANKS = 3
TWICE = (5, 6)
LAST = CHUNKS - 1
REFILL = (LAST,) + TWICE
H_VECTOR = TWICE[0]
EARLY_PASS = 4

EARLY_MOVES = 5
W1_SCALAR = (56, 44)
W2_PARTS = ((0, 48), (48, P))
RUN = 4


def tile_picked_zgrn_lin_po_kernel(tc, x_words, x_scales, w1, w2, offs, out_0, out_1, out_2):
    nc = tc.nc
    with ExitStack() as ctx:
        keep = ctx.enter_context(tc.tile_pool(name="keep", bufs=1))
        ring = ctx.enter_context(tc.tile_pool(name="ring", bufs=CHUNKS))
        psum = ctx.enter_context(tc.psum_pool(name="psum", bufs=1))

        offsets = keep.tile([P, S // LIST_ROWS], U16, name="offsets")
        x_table = [keep.tile([P, T], U32, name="x_table0", tag="first", align_bytes=ALIGN)]
        s_table = keep.tile([P, T], U8, name="s_table", tag="second", align_bytes=ALIGN)
        s_picked = keep.tile([P, S], U8, name="s_picked", align_bytes=ALIGN)
        w1_raw = [keep.tile([P, PACK, H], F32, name="w_raw%d" % g, tag="stage%d" % g, align_bytes=ALIGN) for g in range(PASSES)]
        w_bf = [keep.tile([P, PACK * H], BF16, name="w_bf%d" % g, tag="w_bf%d" % g, align_bytes=ALIGN) for g in range(PASSES + 1)]
        w_codes = [keep.tile([P, H], U32, name="w_codes%d" % g, align_bytes=ALIGN) for g in range(PASSES + 1)]
        w_scales = [keep.tile([P, H], U8, name="w_scales%d" % g, align_bytes=ALIGN) for g in range(PASSES + 1)]
        x_codes = [keep.tile([P, S], U32, name="x_codes%d" % g, align_bytes=ALIGN) for g in range(PASSES)]
        x_planes = [keep.tile([P, S], U8, name="x_planes%d" % g, align_bytes=ALIGN) for g in range(PASSES)]
        y_scales = keep.tile([P, S], U8, name="y_scales", align_bytes=ALIGN)

        x_rows = [x_words[g].rearrange("p n t -> p (n t)").bitcast(I32) for g in range(PASSES)]
        nc.vector.memset(s_table[0 : P - QUADRANT, :].bitcast(I32), 0)
        for g in range(PASSES):
            nc.gpsimd.memset(x_planes[g][:].bitcast(I32), 0)
        nc.sync.dma_start(
            out=s_table[P - QUADRANT : P, :].bitcast(I32), in_=x_scales.rearrange("g r n -> (g r) n").bitcast(I32)
        )
        nc.sync.dma_start(offsets[:], offs)
        nc.sync.dma_start(out=x_table[0][:].bitcast(I32), in_=x_rows[0])
        for g in range(PASSES):
            nc.sync.dma_start(out=w1_raw[g][:], in_=w1[g * K_PASS : (g + 1) * K_PASS, :].rearrange("(p j) c -> p j c", j=PACK))

        nc.vector.tensor_copy(out=s_picked[:], in_=s_table[:].indirect(offsets[:]))

        def place_rows(g, q):
            src = P - QUADRANT + SCALE_ROWS * (QUADRANTS * g + q)
            dst = QUADRANT * q + SCALE_ROWS * g
            nc.sync.dma_start(
                out=x_planes[g][dst : dst + SCALE_ROWS, :].bitcast(I32), in_=s_picked[src : src + SCALE_ROWS, :].bitcast(I32)
            )

        moves = [(g, q) for g in range(PASSES) for q in range(QUADRANTS)]
        for g, q in moves[:EARLY_MOVES]:
            place_rows(g, q)
        x_table.append(keep.tile([P, T], U32, name="x_table1", tag="second", align_bytes=ALIGN))
        nc.sync.dma_start(out=x_table[1][:].bitcast(I32), in_=x_rows[1])
        for g, q in moves[EARLY_MOVES:]:
            place_rows(g, q)

        nc.vector.tensor_copy(out=x_codes[0][:], in_=x_table[0][:].indirect(offsets[:]))
        w2_stage = keep.tile([P, PACK * H], F32, name="w2_stage", tag="first", align_bytes=ALIGN)
        w2_raw = [
            w2_stage[:, PACK * PACK * m0 : PACK * PACK * m1].rearrange("p (j c) -> p j c", j=PACK) for m0, m1 in W2_PARTS
        ]
        for i, (m0, m1) in enumerate(W2_PARTS):
            nc.sync.dma_start(out=w2_raw[i], in_=w2.rearrange("(p j) c -> p j c", j=PACK)[:, :, PACK * m0 : PACK * m1])

        warm = keep.tile([P, 8], F32, name="warm")
        nc.vector.memset(warm[:], 0.0)
        nc.scalar.activation(out=warm[:], in_=warm[:], func=SIGMOID)

        def deal(copy, g, raw, m0, m1, t0=0, t1=PACK):
            dst = w_bf[g][:].rearrange("p (t m j) -> p m j t", t=PACK, j=PACK)[:, m0:m1, :, t0:t1]
            walk = "p (pair e) j t -> p pair j e t"
            copy(out=dst.rearrange(walk, e=2), in_=raw[:, :, :, t0:t1].rearrange(walk, e=2))

        def gpsimd_copy(out, in_):
            nc.gpsimd.tensor_scalar(out=out, in0=in_, scalar1=1.0, scalar2=0.0, op0=MULT, op1=ADD)

        def gpsimd_deal(out, in_):
            walk = "p pair j e t -> p t pair e j"
            gpsimd_copy(out.rearrange(walk), in_.rearrange(walk))

        def by_slice(raw):
            return raw.rearrange("p j (m t) -> p m j t", t=PACK)

        def quantize_w(g, t0, t1):
            nc.vector.quantize_mx(
                out=w_codes[g][:, t0 * P : t1 * P].bitcast(FP8X4),
                scales=w_scales[g][:, t0 * P : t1 * P],
                in_=w_bf[g][:, t0 * K_PASS : t1 * K_PASS],
            )

        for g in range(PASSES):
            split = W1_SCALAR[g]
            for t in range(0, PACK, 2):
                deal(nc.scalar.copy, g, by_slice(w1_raw[g][:])[:, 0:split], 0, split, t, t + 2)
                deal(nc.vector.tensor_copy, g, by_slice(w1_raw[g][:])[:, split:P], split, P, t, t + 2)
            for t in range(0, PACK, 2):
                quantize_w(g, t, t + 2)
        for e0, e1 in PIECES:
            nc.vector.tensor_copy(
                out=x_codes[1][:, e0:e1], in_=x_table[1][:].indirect(offsets[:, e0 // LIST_ROWS : e1 // LIST_ROWS])
            )

        h_ps, z_ps, gate, y = {}, {}, {}, {}
        y_rows = out_0.rearrange("(p t) n -> p t n", t=PACK)
        y_words = out_1[0].rearrange("p n t -> p (n t)").bitcast(I32)

        def tokens(c):
            return slice(c * CHUNK, (c + 1) * CHUNK)

        def values(c):
            return slice(c * CHUNK * PACK, (c + 1) * CHUNK * PACK)

        def bank(b, name):
            return psum.tile([P, PACK, CHUNK], F32, name=name, tag="bank%d" % b)

        def first_product(c, g, opens, b):
            if opens:
                h_ps[c] = bank(b, "h%d_%d" % (c, b))
            for t in range(PACK):
                nc.tensor.matmul_mx(
                    out=h_ps[c][:, t, :],
                    lhsT=w_codes[g][:, t * P : (t + 1) * P].bitcast(FP8X4),
                    lhsT_scale=w_scales[g][:, t * P : (t + 1) * P],
                    rhs=x_codes[g][:, tokens(c)].bitcast(FP8X4),
                    rhs_scale=x_planes[g][SCALE_ROWS * g : P, tokens(c)],
                    start=(opens and t == 0),
                    stop=(not opens and t == PACK - 1),
                )

        def h_bf(c):
            return h_bf_vector[:] if c == H_VECTOR else h_bf_scalar[:, values(c)]

        def round_h(c):
            copy = nc.vector.tensor_copy if c == H_VECTOR else nc.scalar.copy
            copy(
                out=h_bf(c).rearrange("p (n t) -> p n t", t=PACK),
                in_=h_ps[c][:].rearrange("p t n -> p n t"),
            )

        def quantize_h(c):
            nc.vector.quantize_mx(out=h_codes[:, tokens(c)].bitcast(FP8X4), scales=h_scales[:, tokens(c)], in_=h_bf(c))

        def second_product(c):
            z = bank(H_BANKS + c % Z_BANKS, "z%d" % c)
            for t in range(PACK):
                nc.tensor.matmul_mx(
                    out=z[:, t, :],
                    lhsT=w_codes[W2][:, t * P : (t + 1) * P].bitcast(FP8X4),
                    lhsT_scale=w_scales[W2][:, t * P : (t + 1) * P],
                    rhs=h_codes[:, tokens(c)].bitcast(FP8X4),
                    rhs_scale=h_scales[:, tokens(c)],
                    start=True,
                    stop=True,
                )
            z_ps[c] = z

        def sigmoid(c):
            gate[c] = keep.tile([P, PACK, CHUNK], F32, name="gate%d" % c, tag="gate%d" % c, align_bytes=ALIGN)
            nc.scalar.activation(out=gate[c][:], in_=z_ps[c][:], func=SIGMOID)

        def refill(i):
            for g in range(PASSES):
                first_product(REFILL[i], g, g == 0, i)

        def gate_h(c):
            y[c] = ring.tile([P, PACK, CHUNK], F32, name="y", align_bytes=ALIGN)
            nc.vector.tensor_tensor(out=y[c][:], in0=h_ps[c][:], in1=gate[c][:], op=MULT)
            nc.sync.dma_start(out=y_rows[:, :, tokens(c)], in_=y[c][:])

        def round_y(c, dst, copy):
            copy(
                out=dst.rearrange("p (run i t) -> p run t i", i=LINE, t=PACK),
                in_=y[c][:].rearrange("p t (run i) -> p run t i", i=LINE),
            )

        def round_y_gpsimd(c, dst):
            gpsimd_copy(dst.rearrange("p (n t) -> p n t", t=PACK), y[c][:].rearrange("p t n -> p n t"))

        def quantize_y(c0, c1, codes, src):
            nc.vector.quantize_mx(out=codes.bitcast(FP8X4), scales=y_scales[:, c0 * CHUNK : c1 * CHUNK], in_=src)

        def store_codes(c0, c1, codes):
            nc.sync.dma_start(out=y_words[:, c0 * CHUNK : c1 * CHUNK], in_=codes.bitcast(I32))

        deal(gpsimd_deal, W2, by_slice(w2_raw[0]), *W2_PARTS[0])
        h_bf_scalar = keep.tile([P, S * PACK], BF16, name="h_bf", align_bytes=ALIGN)
        for c in range(EARLY_PASS):
            first_product(c, 0, True, c)
        for c in range(LAST):
            b = c + 1 if c in TWICE else c
            first_product(c, 1, c >= EARLY_PASS, b)
            if c >= EARLY_PASS:
                first_product(c, 0, False, b)
            if c != H_VECTOR:
                round_h(c)
        for t in range(0, PACK, 2):
            deal(nc.vector.tensor_copy, W2, by_slice(w2_raw[1]), *W2_PARTS[1], t, t + 2)
        h_codes = keep.tile([P, S], U32, name="h_codes", tag="first", align_bytes=ALIGN)
        h_scales = keep.tile([P, S], U8, name="h_scales", align_bytes=ALIGN)
        for t in range(PACK):
            if t == 2:
                quantize_h(0)
            nc.vector.quantize_mx(
                out=w_codes[W2][:, t * P : (t + 1) * P].bitcast(FP8X4),
                scales=w_scales[W2][:, t * P : (t + 1) * P],
                in_=w_bf[W2][:, t * K_PASS : (t + 1) * K_PASS],
            )
        quantize_h(1)
        h_bf_vector = keep.tile([P, CHUNK * PACK], BF16, name="h_bf_vector", tag="w_bf%d" % W2, align_bytes=ALIGN)
        round_h(H_VECTOR)
        for c in range(2, LAST):
            quantize_h(c)

        def pair(name, tag, dtype, columns):
            return keep.tile([P, 2 * columns], dtype, name=name, tag=tag, align_bytes=ALIGN)

        def finish(c, tag, src):
            codes = pair("y_codes%d" % c, tag, U32, CHUNK)
            quantize_y(c, c + 2, codes[:], src[:])
            store_codes(c, c + 2, codes[:])

        y_bf01 = pair("y_bf01", "y_bf_gpsimd", BF16, CHUNK * PACK)
        for c in range(RUN):
            second_product(c)
            sigmoid(c)
        for c in range(RUN):
            gate_h(c)
            if c < 2:
                round_y_gpsimd(c, y_bf01[:, values(c)])
        refill(0)
        for c in range(RUN, LAST):
            second_product(c)
        refill(1)
        refill(2)
        round_h(LAST)
        quantize_h(LAST)
        finish(0, "gate%d" % (RUN - 1), y_bf01)

        y_bf23 = pair("y_bf23", "y_bf_gpsimd", BF16, CHUNK * PACK)
        for c in range(RUN, CHUNKS):
            if c == LAST:
                second_product(c)
            sigmoid(c)
        for c in range(RUN, CHUNKS):
            gate_h(c)
        for c in (2, 3):
            round_y_gpsimd(c, y_bf23[:, values(c - 2)])
        y_bf45 = pair("y_bf45", "first", BF16, CHUNK * PACK)
        y_bf67 = pair("y_bf67", "y_bf67", BF16, CHUNK * PACK)
        for c in (4, 5):
            round_y(c, y_bf45[:, values(c - 4)], nc.scalar.copy)
        round_y(6, y_bf67[:, values(0)], nc.scalar.copy)
        finish(2, "gate%d" % LAST, y_bf23)
        round_y(LAST, y_bf67[:, values(1)], nc.vector.tensor_copy)
        finish(4, "y_codes4", y_bf45)
        finish(6, "y_codes6", y_bf67)

        for q in range(QUADRANTS):
            queue = nc.sync if q % 2 == 0 else nc.scalar
            queue.dma_start(
                out=out_2[0, SCALE_ROWS * q : SCALE_ROWS * (q + 1), :].bitcast(I32),
                in_=y_scales[QUADRANT * q : QUADRANT * q + SCALE_ROWS, :].bitcast(I32),
            )
